import numpy as np
import ml_dtypes


def mxq(x, axis, fmt="e4m3"):
    dtype, down = {"e4m3": (ml_dtypes.float8_e4m3fn, 7), "e5m2": (ml_dtypes.float8_e5m2, 14)}[fmt]
    v = np.moveaxis(np.asarray(x, np.float32).astype(ml_dtypes.bfloat16).astype(np.float64), axis, -1)
    blocks = v.reshape(v.shape[:-1] + (-1, 32))
    amax = np.abs(blocks).max(-1, keepdims=True)
    byte = np.maximum(np.where(amax > 0, np.frexp(amax)[1] - 1 + 127, 0) - down, 1)
    scale = np.exp2(byte - 127.0)
    codes = (blocks / scale).astype(np.float32).astype(dtype).astype(np.float64)
    return np.moveaxis((codes * scale).reshape(v.shape), -1, axis)


WIDE = False


def mx_kscale(k):
    if not WIDE:
        return np.ones(k)
    levels = np.array([10, -10, 5, -5, 0])
    if k % 512:
        return np.exp2(np.random.permutation(np.resize(levels, k // 32))).repeat(32)
    a = np.empty((k // 512, 16))
    for p in range(k // 512):
        a[p, :8] = np.random.permutation(np.resize(levels, 8))
        for g in range(8):
            far = levels[np.abs(levels - a[p, g]) >= 10]
            a[p, g + 8] = far[np.random.randint(len(far))]
    return np.exp2(a.ravel()).repeat(32)


def f64(x):
    return np.asarray(x).astype(np.float64)


def striped(idx):
    return np.tile(np.asarray(idx).reshape(-1, 16).T, (8, 1)).astype(np.uint16)


def unstriped(offs):
    return offs[:16].T.reshape(-1).astype(np.int64)


E2M1 = np.array([0.0, 0.5, 1.0, 1.5, 2.0, 3.0, 4.0, 6.0, -0.0, -0.5, -1.0, -1.5, -2.0, -3.0, -4.0, -6.0])


def pack_weight(w, fmt):
    k, n = w.shape
    w = f64(np.asarray(w, np.float32).astype(ml_dtypes.bfloat16)).reshape(k // 32, 32, n)
    amax = np.abs(w).max(1)
    if fmt == "e4m3":
        byte = np.frexp(amax)[1] - 1 + 127 - 7
    else:
        mant, ex = np.frexp(amax / 6.0)
        byte = np.where(mant > 0.5, ex, ex - 1) + 127
    byte = np.clip(np.where(amax > 0, byte, 1), 1, 254)
    scaled = (w * np.exp2(127.0 - byte)[:, None, :]).reshape(k, n).astype(np.float32)
    by_word = np.ascontiguousarray(scaled.reshape(k // 512, 128, 4, n).transpose(0, 1, 3, 2))
    if fmt == "e4m3":
        words = by_word.astype(ml_dtypes.float8_e4m3fn).view(np.uint8)
    else:
        c = by_word.astype(ml_dtypes.float4_e2m1fn).view(np.uint8) & 0xF
        words = (c[..., 0::2] | (c[..., 1::2] << 4)).reshape(k // 512, 128, 2 * n)
    return np.ascontiguousarray(words), np.ascontiguousarray(byte.astype(np.uint8).reshape(k // 512, 16, n))


def unpack_weight(words, scales, fmt):
    g, _, n = scales.shape
    words = np.ascontiguousarray(words).reshape(g, 128, n, -1)
    if fmt == "e4m3":
        vals = words.view(ml_dtypes.float8_e4m3fn).astype(np.float64)
    else:
        nib = np.empty((g, 128, n, 4), np.uint8)
        nib[..., 0::2] = words & 0xF
        nib[..., 1::2] = words >> 4
        vals = E2M1[nib]
    vals = vals * np.repeat(np.exp2(scales.astype(np.float64) - 127.0), 8, axis=1)[..., None]
    return vals.transpose(0, 1, 3, 2).reshape(g * 512, n)


D, C, T, I, Q, E = 512, 1024, 2048, 512, 128, 512


def setup_inputs():
    n = np.random.standard_normal
    idx = np.random.randint(0, C, I)
    idx2 = np.random.permutation(T)[:I]
    fd = mx_kscale(D)
    fi = mx_kscale(I)
    ti = np.ones(T)
    ti[idx2] = fi
    bookp = pack_weight(n((D, C)) / fd[:, None], "e4m3")
    return {
        "query": (n((D, Q)) * 0.5 / np.sqrt(D) * fd[:, None]).astype(np.float32),
        "book_words": bookp[0],
        "book_scales": bookp[1],
        "size": (np.random.uniform(0.5, 2.0, (1, I)) * fi).astype(np.float32),
        "vals": (n((E, T)) / ti).astype(np.float32),
        "offs": striped(idx),
        "offs2": striped(idx2),
    }


def reference(query, book_words, book_scales, size, vals, offs, offs2):
    idx = unstriped(offs)
    idx2 = unstriped(offs2)
    booku = unpack_weight(book_words, book_scales, "e4m3")
    queryq = mxq(f64(query), 0, "e4m3")
    b = queryq.T @ booku
    p = np.exp(b[:, idx] - np.max(b[:, idx], axis=1, keepdims=True))
    w = p * f64(size) / np.sum(p, axis=1, keepdims=True)
    wt = w.T
    vt = f64(vals)[:, idx2].T
    wtq = mxq(wt, 0, "e4m3")
    vtq = mxq(vt, 0, "e4m3")
    o = wtq.T @ vtq
    return o

@@ -1,0 +1,168 @@
+from contextlib import ExitStack
+
+import concourse.mybir as mybir
+from concourse.masks import make_identity
+
+D, C, T, I, Q, E = 512, 1024, 2048, 512, 128, 512
+FLOPS = 2 * D * Q * C + 2 * I * Q * E
+
+F32 = mybir.dt.float32
+BF16 = mybir.dt.bfloat16
+I32 = mybir.dt.int32
+U32 = mybir.dt.uint32
+U16 = mybir.dt.uint16
+U8 = mybir.dt.uint8
+FP8X4 = mybir.dt.float8_e4m3fn_x4
+ALU = mybir.AluOpType
+ACT = mybir.ActivationFunctionType
+
+P = 128
+PACK = 4
+BANK = 512
+
+
+def turn(nc, rows, ident, turned, grouped):
+    words = rows[:].bitcast(F32)
+    for u in range(2):
+        nc.tensor.transpose(turned[:, u, :], words[:, u : 2 * P : 2], ident[:])
+    nc.scalar.copy(
+        out=grouped.bitcast(F32).rearrange("p (r u) -> p r u", u=2),
+        in_=turned[:].rearrange("p u r -> p r u"),
+    )
+
+
+def tile_attend_vqattention_kernel(tc, query, book_words, book_scales, size, vals, offs, offs2, out):
+    nc = tc.nc
+    with ExitStack() as ctx:
+        keep = ctx.enter_context(tc.tile_pool(name="keep", bufs=1))
+        psum = ctx.enter_context(tc.psum_pool(name="psum", bufs=1))
+        psum2 = ctx.enter_context(tc.psum_pool(name="psum2", bufs=2))
+
+        code_list = keep.tile([P, I // 16], U16, name="code_list")
+        token_list = keep.tile([P, I // 16], U16, name="token_list")
+        q_raw = keep.tile([P, PACK, Q], F32, name="q_raw")
+        book_codes = keep.tile([P, C], U32, name="book_codes", align_bytes=64)
+        book_plane = keep.tile([P, C], U8, name="book_plane", align_bytes=64)
+        size_col = keep.tile([P, PACK], F32, name="size_col")
+        pools = [keep.tile([P, T], F32, name=f"pool{j}", align_bytes=64) for j in range(E // P)]
+        ident = keep.tile([P, P], F32, name="ident")
+
+        nc.gpsimd.memset(book_plane[:].bitcast(I32), 0)
+        nc.gpsimd.dma_start(out=size_col[:], in_=size[0].rearrange("(p t) -> p t", t=PACK))
+        scale_rows = book_scales[0].bitcast(I32)
+        nc.sync.dma_start(out=q_raw[:], in_=query.rearrange("(p j) q -> p j q", j=PACK))
+        for quad in range(4):
+            nc.sync.dma_start(
+                out=book_plane[32 * quad : 32 * quad + 4, :].bitcast(I32),
+                in_=scale_rows[4 * quad : 4 * quad + 4, :],
+            )
+        nc.sync.dma_start(
+            out=book_codes[:].bitcast(I32),
+            in_=book_words[0].rearrange("p c t -> p (c t)").bitcast(I32),
+        )
+        nc.sync.dma_start(code_list[:], offs)
+        nc.sync.dma_start(out=pools[0][:], in_=vals[0:P, :])
+        nc.sync.dma_start(token_list[:], offs2)
+        for j in range(1, E // P):
+            nc.sync.dma_start(out=pools[j][:], in_=vals[j * P : (j + 1) * P, :])
+        make_identity(nc, ident[:])
+
+        q_grouped = keep.tile([P, Q * PACK], BF16, name="q_grouped", align_bytes=64)
+        q_codes = keep.tile([P, Q], U32, name="q_codes", align_bytes=64)
+        q_plane = keep.tile([P, Q], U8, name="q_plane", align_bytes=64)
+        nc.vector.tensor_copy(
+            out=q_grouped[:].rearrange("p (c i t) -> p c t i", i=4, t=PACK),
+            in_=q_raw[:].rearrange("p t (c i) -> p c t i", i=4),
+        )
+        nc.vector.quantize_mx(out=q_codes[:].bitcast(FP8X4), scales=q_plane[:], in_=q_grouped[:])
+
+        scores = keep.tile([P, C], F32, name="scores")
+        pieces = ((0, 512, nc.scalar.copy), (512, 768, nc.vector.tensor_copy), (768, 1024, nc.scalar.copy))
+        for h, (first, last, copy_out) in enumerate(pieces):
+            cols = slice(first, last)
+            acc = psum.tile([P, last - first], F32, name="score_bank", tag=f"turned{h}")
+            nc.tensor.matmul_mx(
+                out=acc[:],
+                lhsT=q_codes[:].bitcast(FP8X4),
+                lhsT_scale=q_plane[:],
+                rhs=book_codes[:, cols].bitcast(FP8X4),
+                rhs_scale=book_plane[:, cols],
+                start=True,
+                stop=True,
+            )
+            copy_out(out=scores[:, cols], in_=acc[:])
+
+        size_rows = psum.tile([P, PACK, P], F32, name="size_rows", tag="turned3")
+        for t in range(PACK):
+            nc.tensor.transpose(size_rows[:, t, :], size_col[:, t : t + 1].to_broadcast([P, P]), ident[:])
+
+        picked = keep.tile([P, I], F32, name="picked")
+        neg_max = keep.tile([P, 1], F32, name="neg_max")
+        probs = keep.tile([P, I], F32, name="probs", tag="gathered1", align_bytes=64)
+        row_sum = keep.tile([P, 1], F32, name="row_sum")
+        inv_sum = keep.tile([P, 1], F32, name="inv_sum")
+        nc.vector.tensor_copy(out=picked[:], in_=scores[:].indirect(code_list[:]))
+        nc.vector.tensor_reduce(out=neg_max[:], in_=picked[:], axis=mybir.AxisListType.X, op=ALU.max, negate=True)
+        nc.scalar.activation(out=probs[:], in_=picked[:], func=ACT.Exp, bias=neg_max[:], accum_out=row_sum[:])
+
+        gathered = keep.tile([P, I], BF16, name="gathered0", align_bytes=64)
+        nc.vector.tensor_copy(out=gathered[:], in_=pools[0][:].indirect(token_list[:]))
+
+        weights = keep.tile([P, I], BF16, name="weights", align_bytes=64)
+        nc.vector.reciprocal(out=inv_sum[:], in_=row_sum[:])
+        nc.vector.scalar_tensor_tensor(
+            out=weights[:].rearrange("q (s t) -> q s t", t=PACK),
+            in0=probs[:].rearrange("q (s t) -> q s t", t=PACK),
+            scalar=inv_sum[:],
+            in1=size_rows[:].rearrange("q t s -> q s t"),
+            op0=ALU.mult,
+            op1=ALU.mult,
+        )
+        w_turned = psum.tile([P, 2, P], F32, name="w_turned", tag="turned2")
+        w_grouped = keep.tile([P, Q * PACK], BF16, name="w_grouped", tag="gathered3", align_bytes=64)
+        turn(nc, weights, ident, w_turned, w_grouped[:])
+
+        def gather(j):
+            picked_vals = keep.tile([P, I], BF16, name=f"gathered{j}", align_bytes=64)
+            nc.vector.tensor_copy(out=picked_vals[:], in_=pools[j][:].indirect(token_list[:]))
+            return picked_vals
+
+        def turn_vals(j, picked_vals, grouped):
+            v_turned = psum.tile([P, 2, P], F32, name="v_turned", tag=f"turned{j}")
+            turn(nc, picked_vals, ident, v_turned, grouped)
+
+        def quantise(grouped, name, tag):
+            width = grouped.shape[1] // PACK
+            codes = keep.tile([P, width], U32, name=f"{name}_codes", tag=tag, align_bytes=64)
+            plane = keep.tile([P, width], U8, name=f"{name}_plane", align_bytes=64)
+            nc.vector.quantize_mx(out=codes[:].bitcast(FP8X4), scales=plane[:], in_=grouped[:])
+            return codes, plane
+
+        def multiply(first, w_mx, v_mx):
+            width = v_mx[0].shape[1]
+            o_bank = psum2.tile([P, width], F32, name="o_bank")
+            nc.tensor.matmul_mx(
+                out=o_bank[:],
+                lhsT=w_mx[0][:].bitcast(FP8X4),
+                lhsT_scale=w_mx[1][:],
+                rhs=v_mx[0][:].bitcast(FP8X4),
+                rhs_scale=v_mx[1][:],
+                start=True,
+                stop=True,
+            )
+            result = keep.tile([P, width], F32, name=f"result{first}")
+            nc.scalar.copy(out=result[:], in_=o_bank[:])
+            nc.sync.dma_start(out=out[:, first : first + width], in_=result[:])
+
+        grouped01 = keep.tile([P, 2 * I], BF16, name="grouped01", align_bytes=64)
+        grouped2 = keep.tile([P, I], BF16, name="grouped2", align_bytes=64)
+        grouped3 = keep.tile([P, I], BF16, name="grouped3", align_bytes=64)
+        turn_vals(0, gathered, grouped01[:, :I])
+        turn_vals(1, gather(1), grouped01[:, I:])
+        turn_vals(2, gather(2), grouped2[:])
+        v01 = quantise(grouped01, "v01", "pool2")
+        w_mx = quantise(w_grouped, "w", "grouped01")
+        multiply(0, w_mx, v01)
+        turn_vals(3, gather(3), grouped3[:])
+        multiply(2 * P, w_mx, quantise(grouped2, "v2", "pool3"))
+        multiply(3 * P, w_mx, quantise(grouped3, "v3", "v3_codes"))

@@ -98,15 +98,20 @@ def tile_attend_vqattention_kernel(tc, query, book_words, book_scales, size, val
 
         picked = keep.tile([P, I], F32, name="picked")
         neg_max = keep.tile([P, 1], F32, name="neg_max")
-        probs = keep.tile([P, I], F32, name="probs", tag="gathered1", align_bytes=64)
+        probs = keep.tile([P, I], F32, name="probs", tag="gathered2", align_bytes=64)
         row_sum = keep.tile([P, 1], F32, name="row_sum")
-        inv_sum = keep.tile([P, 1], F32, name="inv_sum")
         nc.vector.tensor_copy(out=picked[:], in_=scores[:].indirect(code_list[:]))
         nc.vector.tensor_reduce(out=neg_max[:], in_=picked[:], axis=mybir.AxisListType.X, op=ALU.max, negate=True)
         nc.scalar.activation(out=probs[:], in_=picked[:], func=ACT.Exp, bias=neg_max[:], accum_out=row_sum[:])
 
-        gathered = keep.tile([P, I], BF16, name="gathered0", align_bytes=64)
-        nc.vector.tensor_copy(out=gathered[:], in_=pools[0][:].indirect(token_list[:]))
+        def gather(j):
+            picked_vals = keep.tile([P, I], BF16, name=f"gathered{j}", align_bytes=64)
+            nc.vector.tensor_copy(out=picked_vals[:], in_=pools[j][:].indirect(token_list[:]))
+            return picked_vals
+
+        gathered0 = gather(0)
+        gathered1 = gather(1)
+        inv_sum = keep.tile([P, 1], F32, name="inv_sum", tag="pool1", align_bytes=64)
 
         weights = keep.tile([P, I], BF16, name="weights", align_bytes=64)
         nc.vector.reciprocal(out=inv_sum[:], in_=row_sum[:])
@@ -121,11 +126,6 @@ def tile_attend_vqattention_kernel(tc, query, book_words, book_scales, size, val
         w_turned = psum.tile([P, 2, P], F32, name="w_turned", tag="turned2")
         w_grouped = keep.tile([P, Q * PACK], BF16, name="w_grouped", tag="gathered3", align_bytes=64)
         turn(nc, weights, ident, w_turned, w_grouped[:])
-
-        def gather(j):
-            picked_vals = keep.tile([P, I], BF16, name=f"gathered{j}", align_bytes=64)
-            nc.vector.tensor_copy(out=picked_vals[:], in_=pools[j][:].indirect(token_list[:]))
-            return picked_vals
 
         def turn_vals(j, picked_vals, grouped):
             v_turned = psum.tile([P, 2, P], F32, name="v_turned", tag=f"turned{j}")
@@ -157,8 +157,8 @@ def tile_attend_vqattention_kernel(tc, query, book_words, book_scales, size, val
         grouped01 = keep.tile([P, 2 * I], BF16, name="grouped01", align_bytes=64)
         grouped2 = keep.tile([P, I], BF16, name="grouped2", align_bytes=64)
         grouped3 = keep.tile([P, I], BF16, name="grouped3", align_bytes=64)
-        turn_vals(0, gathered, grouped01[:, :I])
-        turn_vals(1, gather(1), grouped01[:, I:])
+        turn_vals(0, gathered0, grouped01[:, :I])
+        turn_vals(1, gathered1, grouped01[:, I:])
         turn_vals(2, gather(2), grouped2[:])
         v01 = quantise(grouped01, "v01", "pool2")
         w_mx = quantise(w_grouped, "w", "grouped01")

@@ -36,7 +36,6 @@ def tile_attend_vqattention_kernel(tc, query, book_words, book_scales, size, val
     with ExitStack() as ctx:
         keep = ctx.enter_context(tc.tile_pool(name="keep", bufs=1))
         psum = ctx.enter_context(tc.psum_pool(name="psum", bufs=1))
-        psum2 = ctx.enter_context(tc.psum_pool(name="psum2", bufs=2))
 
         code_list = keep.tile([P, I // 16], U16, name="code_list")
         token_list = keep.tile([P, I // 16], U16, name="token_list")
@@ -96,21 +95,25 @@ def tile_attend_vqattention_kernel(tc, query, book_words, book_scales, size, val
         for t in range(PACK):
             nc.tensor.transpose(size_rows[:, t, :], size_col[:, t : t + 1].to_broadcast([P, P]), ident[:])
 
-        picked = keep.tile([P, I], F32, name="picked")
+        pool0_bf16 = keep.tile([P, T], BF16, name="pool0_bf16", align_bytes=64)
+        nc.scalar.activation(out=pool0_bf16[:], in_=pools[0][:], func=ACT.Copy)
+
+        picked = keep.tile([P, I], F32, name="picked", tag="gathered0", align_bytes=64)
         neg_max = keep.tile([P, 1], F32, name="neg_max")
-        probs = keep.tile([P, I], F32, name="probs", tag="gathered2", align_bytes=64)
+        probs = keep.tile([P, I], F32, name="probs", tag="pool0", align_bytes=64)
         row_sum = keep.tile([P, 1], F32, name="row_sum")
         nc.vector.tensor_copy(out=picked[:], in_=scores[:].indirect(code_list[:]))
         nc.vector.tensor_reduce(out=neg_max[:], in_=picked[:], axis=mybir.AxisListType.X, op=ALU.max, negate=True)
         nc.scalar.activation(out=probs[:], in_=picked[:], func=ACT.Exp, bias=neg_max[:], accum_out=row_sum[:])
 
-        def gather(j):
-            picked_vals = keep.tile([P, I], BF16, name=f"gathered{j}", align_bytes=64)
+        def gather(j, tag):
+            picked_vals = keep.tile([P, I], BF16, name=f"gathered{j}", tag=tag, align_bytes=64)
             nc.vector.tensor_copy(out=picked_vals[:], in_=pools[j][:].indirect(token_list[:]))
             return picked_vals
 
-        gathered0 = gather(0)
-        gathered1 = gather(1)
+        gathered0 = keep.tile([P, I], BF16, name="gathered0", align_bytes=64)
+        nc.scalar.activation(out=gathered0[:], in_=pool0_bf16[:].indirect(token_list[:]), func=ACT.Copy)
+        gathered1 = gather(1, "gathered1")
         inv_sum = keep.tile([P, 1], F32, name="inv_sum", tag="pool1", align_bytes=64)
 
         weights = keep.tile([P, I], BF16, name="weights", align_bytes=64)
@@ -123,13 +126,10 @@ def tile_attend_vqattention_kernel(tc, query, book_words, book_scales, size, val
             op0=ALU.mult,
             op1=ALU.mult,
         )
-        w_turned = psum.tile([P, 2, P], F32, name="w_turned", tag="turned2")
-        w_grouped = keep.tile([P, Q * PACK], BF16, name="w_grouped", tag="gathered3", align_bytes=64)
-        turn(nc, weights, ident, w_turned, w_grouped[:])
 
-        def turn_vals(j, picked_vals, grouped):
-            v_turned = psum.tile([P, 2, P], F32, name="v_turned", tag=f"turned{j}")
-            turn(nc, picked_vals, ident, v_turned, grouped)
+        def turn_rows(bank, rows, grouped):
+            turned = psum.tile([P, 2, P], F32, name="turned", tag=bank)
+            turn(nc, rows, ident, turned, grouped)
 
         def quantise(grouped, name, tag):
             width = grouped.shape[1] // PACK
@@ -138,31 +138,36 @@ def tile_attend_vqattention_kernel(tc, query, book_words, book_scales, size, val
             nc.vector.quantize_mx(out=codes[:].bitcast(FP8X4), scales=plane[:], in_=grouped[:])
             return codes, plane
 
-        def multiply(first, w_mx, v_mx):
-            width = v_mx[0].shape[1]
-            o_bank = psum2.tile([P, width], F32, name="o_bank")
+        def multiply(acc, w_mx, v_mx, cols):
             nc.tensor.matmul_mx(
-                out=o_bank[:],
-                lhsT=w_mx[0][:].bitcast(FP8X4),
-                lhsT_scale=w_mx[1][:],
-                rhs=v_mx[0][:].bitcast(FP8X4),
-                rhs_scale=v_mx[1][:],
+                out=acc,
+                lhsT=w_mx[0][:, :Q].bitcast(FP8X4),
+                lhsT_scale=w_mx[1][:, :Q],
+                rhs=v_mx[0][:, cols].bitcast(FP8X4),
+                rhs_scale=v_mx[1][:, cols],
                 start=True,
                 stop=True,
             )
+
+        def store(acc, first, copy_out):
+            width = acc.shape[1]
             result = keep.tile([P, width], F32, name=f"result{first}")
-            nc.scalar.copy(out=result[:], in_=o_bank[:])
+            copy_out(out=result[:], in_=acc[:])
             nc.sync.dma_start(out=out[:, first : first + width], in_=result[:])
 
-        grouped01 = keep.tile([P, 2 * I], BF16, name="grouped01", align_bytes=64)
-        grouped2 = keep.tile([P, I], BF16, name="grouped2", align_bytes=64)
-        grouped3 = keep.tile([P, I], BF16, name="grouped3", align_bytes=64)
-        turn_vals(0, gathered0, grouped01[:, :I])
-        turn_vals(1, gathered1, grouped01[:, I:])
-        turn_vals(2, gather(2), grouped2[:])
-        v01 = quantise(grouped01, "v01", "pool2")
-        w_mx = quantise(w_grouped, "w", "grouped01")
-        multiply(0, w_mx, v01)
-        turn_vals(3, gather(3), grouped3[:])
-        multiply(2 * P, w_mx, quantise(grouped2, "v2", "pool3"))
-        multiply(3 * P, w_mx, quantise(grouped3, "v3", "v3_codes"))
+        early = keep.tile([P, 4 * I], BF16, name="early", tag="pool0_bf16", align_bytes=64)
+        late = keep.tile([P, I], BF16, name="late", align_bytes=64)
+        turn_rows("turned1", gathered1, early[:, 2 * I : 3 * I])
+        turn_rows("turned2", weights, early[:, :I])
+        turn_rows("turned2", gathered0, early[:, I : 2 * I])
+        turn_rows("turned0", gather(2, "gathered2"), early[:, 3 * I :])
+        turn_rows("turned3", gather(3, "pool0"), late[:])
+        early_mx = quantise(early, "early", "pool3")
+        early_out = psum.tile([P, 3 * P], F32, name="early_out")
+        multiply(early_out[:, : 2 * P], early_mx, early_mx, slice(P, 3 * P))
+        multiply(early_out[:, 2 * P :], early_mx, early_mx, slice(3 * P, 4 * P))
+        store(early_out, 0, nc.scalar.copy)
+        late_mx = quantise(late, "late", "late_codes")
+        late_out = psum.tile([P, P], F32, name="late_out")
+        multiply(late_out[:], early_mx, late_mx, slice(0, P))
+        store(late_out, 3 * P, nc.vector.tensor_copy)

@@ -50,15 +50,15 @@ def tile_attend_vqattention_kernel(tc, query, book_words, book_scales, size, val
         nc.gpsimd.dma_start(out=size_col[:], in_=size[0].rearrange("(p t) -> p t", t=PACK))
         scale_rows = book_scales[0].bitcast(I32)
         nc.sync.dma_start(out=q_raw[:], in_=query.rearrange("(p j) q -> p j q", j=PACK))
+        nc.sync.dma_start(
+            out=book_codes[:].bitcast(I32),
+            in_=book_words[0].rearrange("p c t -> p (c t)").bitcast(I32),
+        )
         for quad in range(4):
             nc.sync.dma_start(
                 out=book_plane[32 * quad : 32 * quad + 4, :].bitcast(I32),
                 in_=scale_rows[4 * quad : 4 * quad + 4, :],
             )
-        nc.sync.dma_start(
-            out=book_codes[:].bitcast(I32),
-            in_=book_words[0].rearrange("p c t -> p (c t)").bitcast(I32),
-        )
         nc.sync.dma_start(code_list[:], offs)
         nc.sync.dma_start(out=pools[0][:], in_=vals[0:P, :])
         nc.sync.dma_start(token_list[:], offs2)
@@ -163,10 +163,12 @@ def tile_attend_vqattention_kernel(tc, query, book_words, book_scales, size, val
         turn_rows("turned0", gather(2, "gathered2"), early[:, 3 * I :])
         turn_rows("turned3", gather(3, "pool0"), late[:])
         early_mx = quantise(early, "early", "pool3")
-        early_out = psum.tile([P, 3 * P], F32, name="early_out")
-        multiply(early_out[:, : 2 * P], early_mx, early_mx, slice(P, 3 * P))
-        multiply(early_out[:, 2 * P :], early_mx, early_mx, slice(3 * P, 4 * P))
-        store(early_out, 0, nc.scalar.copy)
+        out01 = psum.tile([P, 2 * P], F32, name="out01")
+        multiply(out01[:], early_mx, early_mx, slice(P, 3 * P))
+        store(out01, 0, nc.scalar.copy)
+        out2 = psum.tile([P, P], F32, name="out2")
+        multiply(out2[:], early_mx, early_mx, slice(3 * P, 4 * P))
+        store(out2, 2 * P, nc.scalar.copy)
         late_mx = quantise(late, "late", "late_codes")
         late_out = psum.tile([P, P], F32, name="late_out")
         multiply(late_out[:], early_mx, late_mx, slice(0, P))

@@ -18,7 +18,8 @@ ACT = mybir.ActivationFunctionType
 
 P = 128
 PACK = 4
-BANK = 512
+HALF = P // 2
+POOL_BYTES = 4 * T
 
 
 def turn(nc, rows, ident, turned, grouped):
@@ -35,6 +36,7 @@ def tile_attend_vqattention_kernel(tc, query, book_words, book_scales, size, val
     nc = tc.nc
     with ExitStack() as ctx:
         keep = ctx.enter_context(tc.tile_pool(name="keep", bufs=1))
+        shared = ctx.enter_context(tc.tile_pool(name="shared", bufs=1))
         psum = ctx.enter_context(tc.psum_pool(name="psum", bufs=1))
 
         code_list = keep.tile([P, I // 16], U16, name="code_list")
@@ -43,7 +45,7 @@ def tile_attend_vqattention_kernel(tc, query, book_words, book_scales, size, val
         book_codes = keep.tile([P, C], U32, name="book_codes", align_bytes=64)
         book_plane = keep.tile([P, C], U8, name="book_plane", align_bytes=64)
         size_col = keep.tile([P, PACK], F32, name="size_col")
-        pools = [keep.tile([P, T], F32, name=f"pool{j}", align_bytes=64) for j in range(E // P)]
+        pools = [shared.tile([P, T], F32, name=f"pool{j}", offset=j * POOL_BYTES) for j in range(E // P)]
         ident = keep.tile([P, P], F32, name="ident")
 
         nc.gpsimd.memset(book_plane[:].bitcast(I32), 0)
@@ -60,10 +62,10 @@ def tile_attend_vqattention_kernel(tc, query, book_words, book_scales, size, val
                 in_=scale_rows[4 * quad : 4 * quad + 4, :],
             )
         nc.sync.dma_start(code_list[:], offs)
-        nc.sync.dma_start(out=pools[0][:], in_=vals[0:P, :])
+        nc.sync.dma_start(out=pools[0][:], in_=vals[P : 2 * P, :])
         nc.sync.dma_start(token_list[:], offs2)
-        for j in range(1, E // P):
-            nc.sync.dma_start(out=pools[j][:], in_=vals[j * P : (j + 1) * P, :])
+        for j, block in ((1, 0), (2, 2), (3, 3)):
+            nc.sync.dma_start(out=pools[j][:], in_=vals[block * P : (block + 1) * P, :])
         make_identity(nc, ident[:])
 
         q_grouped = keep.tile([P, Q * PACK], BF16, name="q_grouped", align_bytes=64)
@@ -79,7 +81,7 @@ def tile_attend_vqattention_kernel(tc, query, book_words, book_scales, size, val
         pieces = ((0, 512, nc.scalar.copy), (512, 768, nc.vector.tensor_copy), (768, 1024, nc.scalar.copy))
         for h, (first, last, copy_out) in enumerate(pieces):
             cols = slice(first, last)
-            acc = psum.tile([P, last - first], F32, name="score_bank", tag=f"turned{h}")
+            acc = psum.tile([P, last - first], F32, name="score_bank", tag=f"bank{h}")
             nc.tensor.matmul_mx(
                 out=acc[:],
                 lhsT=q_codes[:].bitcast(FP8X4),
@@ -91,7 +93,7 @@ def tile_attend_vqattention_kernel(tc, query, book_words, book_scales, size, val
             )
             copy_out(out=scores[:, cols], in_=acc[:])
 
-        size_rows = psum.tile([P, PACK, P], F32, name="size_rows", tag="turned3")
+        size_rows = psum.tile([P, PACK, P], F32, name="size_rows", tag="bank3")
         for t in range(PACK):
             nc.tensor.transpose(size_rows[:, t, :], size_col[:, t : t + 1].to_broadcast([P, P]), ident[:])
 
@@ -100,21 +102,20 @@ def tile_attend_vqattention_kernel(tc, query, book_words, book_scales, size, val
 
         picked = keep.tile([P, I], F32, name="picked", tag="gathered0", align_bytes=64)
         neg_max = keep.tile([P, 1], F32, name="neg_max")
-        probs = keep.tile([P, I], F32, name="probs", tag="pool0", align_bytes=64)
+        probs = shared.tile([P, I], F32, name="probs", offset=0)
         row_sum = keep.tile([P, 1], F32, name="row_sum")
         nc.vector.tensor_copy(out=picked[:], in_=scores[:].indirect(code_list[:]))
         nc.vector.tensor_reduce(out=neg_max[:], in_=picked[:], axis=mybir.AxisListType.X, op=ALU.max, negate=True)
         nc.scalar.activation(out=probs[:], in_=picked[:], func=ACT.Exp, bias=neg_max[:], accum_out=row_sum[:])
 
-        def gather(j, tag):
-            picked_vals = keep.tile([P, I], BF16, name=f"gathered{j}", tag=tag, align_bytes=64)
+        def gather(j, picked_vals):
             nc.vector.tensor_copy(out=picked_vals[:], in_=pools[j][:].indirect(token_list[:]))
             return picked_vals
 
         gathered0 = keep.tile([P, I], BF16, name="gathered0", align_bytes=64)
         nc.scalar.activation(out=gathered0[:], in_=pool0_bf16[:].indirect(token_list[:]), func=ACT.Copy)
-        gathered1 = gather(1, "gathered1")
-        inv_sum = keep.tile([P, 1], F32, name="inv_sum", tag="pool1", align_bytes=64)
+        gathered1 = gather(1, keep.tile([P, I], BF16, name="gathered1", align_bytes=64))
+        inv_sum = shared.tile([P, 1], F32, name="inv_sum", offset=POOL_BYTES)
 
         weights = keep.tile([P, I], BF16, name="weights", align_bytes=64)
         nc.vector.reciprocal(out=inv_sum[:], in_=row_sum[:])
@@ -131,11 +132,11 @@ def tile_attend_vqattention_kernel(tc, query, book_words, book_scales, size, val
             turned = psum.tile([P, 2, P], F32, name="turned", tag=bank)
             turn(nc, rows, ident, turned, grouped)
 
-        def quantise(grouped, name, tag):
+        def quantise(grouped, name, offset):
             width = grouped.shape[1] // PACK
-            codes = keep.tile([P, width], U32, name=f"{name}_codes", tag=tag, align_bytes=64)
+            codes = shared.tile([P, width], U32, name=f"{name}_codes", offset=offset, align_bytes=64)
             plane = keep.tile([P, width], U8, name=f"{name}_plane", align_bytes=64)
-            nc.vector.quantize_mx(out=codes[:].bitcast(FP8X4), scales=plane[:], in_=grouped[:])
+            nc.vector.quantize_mx(out=codes[:].bitcast(FP8X4), scales=plane[:], in_=grouped)
             return codes, plane
 
         def multiply(acc, w_mx, v_mx, cols):
@@ -155,21 +156,37 @@ def tile_attend_vqattention_kernel(tc, query, book_words, book_scales, size, val
             copy_out(out=result[:], in_=acc[:])
             nc.sync.dma_start(out=out[:, first : first + width], in_=result[:])
 
-        early = keep.tile([P, 4 * I], BF16, name="early", tag="pool0_bf16", align_bytes=64)
-        late = keep.tile([P, I], BF16, name="late", align_bytes=64)
-        turn_rows("turned1", gathered1, early[:, 2 * I : 3 * I])
-        turn_rows("turned2", weights, early[:, :I])
-        turn_rows("turned2", gathered0, early[:, I : 2 * I])
-        turn_rows("turned0", gather(2, "gathered2"), early[:, 3 * I :])
-        turn_rows("turned3", gather(3, "pool0"), late[:])
-        early_mx = quantise(early, "early", "pool3")
-        out01 = psum.tile([P, 2 * P], F32, name="out01")
-        multiply(out01[:], early_mx, early_mx, slice(P, 3 * P))
-        store(out01, 0, nc.scalar.copy)
-        out2 = psum.tile([P, P], F32, name="out2")
-        multiply(out2[:], early_mx, early_mx, slice(3 * P, 4 * P))
-        store(out2, 2 * P, nc.scalar.copy)
-        late_mx = quantise(late, "late", "late_codes")
-        late_out = psum.tile([P, P], F32, name="late_out")
-        multiply(late_out[:], early_mx, late_mx, slice(0, P))
-        store(late_out, 3 * P, nc.vector.tensor_copy)
+        grouped = keep.tile([P, 4 * I], BF16, name="grouped", tag="pool0_bf16", align_bytes=64)
+        turn_rows("bank1", gathered1, grouped[:, I : 2 * I])
+        turn_rows("bank2", weights, grouped[:, :I])
+        turn_rows("bank3", gathered0, grouped[:, 2 * I : 3 * I])
+        gathered2 = gather(2, keep.tile([P, I], BF16, name="gathered2", align_bytes=64))
+        turn_rows("bank0", gathered2, grouped[:, 3 * I :])
+        w1_mx = quantise(grouped[:, : 2 * I], "w1", 2 * POOL_BYTES)
+        out0 = psum.tile([P, P], F32, name="out0", tag="bank4")
+        multiply(out0[:], w1_mx, w1_mx, slice(P, 2 * P))
+        store(out0, 0, nc.scalar.copy)
+        gathered3 = gather(3, shared.tile([P, I], BF16, name="gathered3", offset=0))
+        words = gathered3[:].bitcast(F32)
+        turned = psum.tile([P, 2, P], F32, name="turned", tag="bank1")
+        for u in range(2):
+            nc.tensor.transpose(turned[:, u, :], words[:, u : 2 * P : 2], ident[:])
+        halves = []
+        for h in range(2):
+            late = keep.tile([P, I // 2], BF16, name=f"late{h}", align_bytes=64)
+            nc.scalar.copy(
+                out=late[:].bitcast(F32).rearrange("p (r u) -> p r u", u=2),
+                in_=turned[:, :, h * HALF : (h + 1) * HALF].rearrange("p u r -> p r u"),
+            )
+            halves.append(late)
+        mid_mx = quantise(grouped[:, 2 * I :], "mid", 3 * POOL_BYTES)
+        out12 = psum.tile([P, 2 * P], F32, name="out12", tag="bank5")
+        multiply(out12[:], w1_mx, mid_mx, slice(0, 2 * P))
+        store(out12, P, nc.scalar.copy)
+        last = keep.tile([P, P], F32, name="last")
+        for h, copy_out in enumerate((nc.scalar.copy, nc.vector.tensor_copy)):
+            late_mx = quantise(halves[h][:], f"late{h}", 4 * POOL_BYTES + 256 * h)
+            late_out = psum.tile([P, HALF], F32, name=f"late_out{h}")
+            multiply(late_out[:], w1_mx, late_mx, slice(0, HALF))
+            copy_out(out=last[:, h * HALF : (h + 1) * HALF], in_=late_out[:])
+        nc.sync.dma_start(out=out[:, 3 * P :], in_=last[:])

@@ -19,6 +19,7 @@ ACT = mybir.ActivationFunctionType
 P = 128
 PACK = 4
 HALF = P // 2
+CHUNKS = I // P
 POOL_BYTES = 4 * T
 
 
@@ -44,12 +45,12 @@ def tile_attend_vqattention_kernel(tc, query, book_words, book_scales, size, val
         q_raw = keep.tile([P, PACK, Q], F32, name="q_raw")
         book_codes = keep.tile([P, C], U32, name="book_codes", align_bytes=64)
         book_plane = keep.tile([P, C], U8, name="book_plane", align_bytes=64)
-        size_col = keep.tile([P, PACK], F32, name="size_col")
+        size_chunks = keep.tile([P, P], F32, name="size_chunks")
         pools = [shared.tile([P, T], F32, name=f"pool{j}", offset=j * POOL_BYTES) for j in range(E // P)]
         ident = keep.tile([P, P], F32, name="ident")
 
         nc.gpsimd.memset(book_plane[:].bitcast(I32), 0)
-        nc.gpsimd.dma_start(out=size_col[:], in_=size[0].rearrange("(p t) -> p t", t=PACK))
+        nc.gpsimd.memset(size_chunks[:], 0.0)
         scale_rows = book_scales[0].bitcast(I32)
         nc.sync.dma_start(out=q_raw[:], in_=query.rearrange("(p j) q -> p j q", j=PACK))
         nc.sync.dma_start(
@@ -63,9 +64,11 @@ def tile_attend_vqattention_kernel(tc, query, book_words, book_scales, size, val
             )
         nc.sync.dma_start(code_list[:], offs)
         nc.sync.dma_start(out=pools[0][:], in_=vals[P : 2 * P, :])
+        nc.sync.dma_start(out=size_chunks[:CHUNKS, :], in_=size[0].rearrange("(c m) -> c m", m=P))
+        nc.sync.dma_start(out=pools[1][:], in_=vals[0:P, :])
         nc.sync.dma_start(token_list[:], offs2)
-        for j, block in ((1, 0), (2, 2), (3, 3)):
-            nc.sync.dma_start(out=pools[j][:], in_=vals[block * P : (block + 1) * P, :])
+        for j in (2, 3):
+            nc.sync.dma_start(out=pools[j][:], in_=vals[j * P : (j + 1) * P, :])
         make_identity(nc, ident[:])
 
         q_grouped = keep.tile([P, Q * PACK], BF16, name="q_grouped", align_bytes=64)
@@ -93,9 +96,13 @@ def tile_attend_vqattention_kernel(tc, query, book_words, book_scales, size, val
             )
             copy_out(out=scores[:, cols], in_=acc[:])
 
-        size_rows = psum.tile([P, PACK, P], F32, name="size_rows", tag="bank3")
-        for t in range(PACK):
-            nc.tensor.transpose(size_rows[:, t, :], size_col[:, t : t + 1].to_broadcast([P, P]), ident[:])
+        size_turned = psum.tile([P, P], F32, name="size_turned", tag="bank3")
+        nc.tensor.transpose(size_turned[:], size_chunks[:], ident[:])
+        size_col = keep.tile([P, CHUNKS], F32, name="size_col")
+        nc.scalar.copy(out=size_col[:], in_=size_turned[:, :CHUNKS])
+        size_rows = psum.tile([P, CHUNKS, P], F32, name="size_rows", tag="bank0")
+        for c in range(CHUNKS):
+            nc.tensor.transpose(size_rows[:, c, :], size_col[:, c : c + 1].to_broadcast([P, P]), ident[:])
 
         pool0_bf16 = keep.tile([P, T], BF16, name="pool0_bf16", align_bytes=64)
         nc.scalar.activation(out=pool0_bf16[:], in_=pools[0][:], func=ACT.Copy)
@@ -120,10 +127,10 @@ def tile_attend_vqattention_kernel(tc, query, book_words, book_scales, size, val
         weights = keep.tile([P, I], BF16, name="weights", align_bytes=64)
         nc.vector.reciprocal(out=inv_sum[:], in_=row_sum[:])
         nc.vector.scalar_tensor_tensor(
-            out=weights[:].rearrange("q (s t) -> q s t", t=PACK),
-            in0=probs[:].rearrange("q (s t) -> q s t", t=PACK),
+            out=weights[:],
+            in0=probs[:],
             scalar=inv_sum[:],
-            in1=size_rows[:].rearrange("q t s -> q s t"),
+            in1=size_rows[:].rearrange("q c m -> q (c m)"),
             op0=ALU.mult,
             op1=ALU.mult,
         )
@@ -159,9 +166,9 @@ def tile_attend_vqattention_kernel(tc, query, book_words, book_scales, size, val
         grouped = keep.tile([P, 4 * I], BF16, name="grouped", tag="pool0_bf16", align_bytes=64)
         turn_rows("bank1", gathered1, grouped[:, I : 2 * I])
         turn_rows("bank2", weights, grouped[:, :I])
-        turn_rows("bank3", gathered0, grouped[:, 2 * I : 3 * I])
+        turn_rows("bank0", gathered0, grouped[:, 2 * I : 3 * I])
         gathered2 = gather(2, keep.tile([P, I], BF16, name="gathered2", align_bytes=64))
-        turn_rows("bank0", gathered2, grouped[:, 3 * I :])
+        turn_rows("bank3", gathered2, grouped[:, 3 * I :])
         w1_mx = quantise(grouped[:, : 2 * I], "w1", 2 * POOL_BYTES)
         out0 = psum.tile([P, P], F32, name="out0", tag="bank4")
         multiply(out0[:], w1_mx, w1_mx, slice(P, 2 * P))

@@ -23,10 +23,14 @@ CHUNKS = I // P
 POOL_BYTES = 4 * T
 
 
+def dealt(rows):
+    return rows.rearrange("p (u b j) -> p b u j", u=2, j=16)
+
+
 def turn(nc, rows, ident, turned, grouped):
     words = rows[:].bitcast(F32)
     for u in range(2):
-        nc.tensor.transpose(turned[:, u, :], words[:, u : 2 * P : 2], ident[:])
+        nc.tensor.transpose(turned[:, u, :], words[:, u * P : (u + 1) * P], ident[:])
     nc.scalar.copy(
         out=grouped.bitcast(F32).rearrange("p (r u) -> p r u", u=2),
         in_=turned[:].rearrange("p u r -> p r u"),
@@ -100,9 +104,9 @@ def tile_attend_vqattention_kernel(tc, query, book_words, book_scales, size, val
         nc.tensor.transpose(size_turned[:], size_chunks[:], ident[:])
         size_col = keep.tile([P, CHUNKS], F32, name="size_col")
         nc.scalar.copy(out=size_col[:], in_=size_turned[:, :CHUNKS])
-        size_rows = psum.tile([P, CHUNKS, P], F32, name="size_rows", tag="bank0")
+        size_rows = psum.tile([P, I], F32, name="size_rows", tag="bank0")
         for c in range(CHUNKS):
-            nc.tensor.transpose(size_rows[:, c, :], size_col[:, c : c + 1].to_broadcast([P, P]), ident[:])
+            nc.tensor.transpose(dealt(size_rows[:])[:, 4 * c : 4 * c + 4], size_col[:, c : c + 1].to_broadcast([P, P]), ident[:])
 
         pool0_bf16 = keep.tile([P, T], BF16, name="pool0_bf16", align_bytes=64)
         nc.scalar.activation(out=pool0_bf16[:], in_=pools[0][:], func=ACT.Copy)
@@ -113,14 +117,14 @@ def tile_attend_vqattention_kernel(tc, query, book_words, book_scales, size, val
         row_sum = keep.tile([P, 1], F32, name="row_sum")
         nc.vector.tensor_copy(out=picked[:], in_=scores[:].indirect(code_list[:]))
         nc.vector.tensor_reduce(out=neg_max[:], in_=picked[:], axis=mybir.AxisListType.X, op=ALU.max, negate=True)
-        nc.scalar.activation(out=probs[:], in_=picked[:], func=ACT.Exp, bias=neg_max[:], accum_out=row_sum[:])
+        nc.scalar.activation(out=dealt(probs[:]), in_=picked[:].rearrange("p (b u j) -> p b u j", u=2, j=16), func=ACT.Exp, bias=neg_max[:], accum_out=row_sum[:])
 
         def gather(j, picked_vals):
-            nc.vector.tensor_copy(out=picked_vals[:], in_=pools[j][:].indirect(token_list[:]))
+            nc.vector.tensor_copy(out=dealt(picked_vals[:]), in_=pools[j][:].indirect(token_list[:]))
             return picked_vals
 
         gathered0 = keep.tile([P, I], BF16, name="gathered0", align_bytes=64)
-        nc.scalar.activation(out=gathered0[:], in_=pool0_bf16[:].indirect(token_list[:]), func=ACT.Copy)
+        nc.scalar.activation(out=dealt(gathered0[:]), in_=pool0_bf16[:].indirect(token_list[:]), func=ACT.Copy)
         gathered1 = gather(1, keep.tile([P, I], BF16, name="gathered1", align_bytes=64))
         inv_sum = shared.tile([P, 1], F32, name="inv_sum", offset=POOL_BYTES)
 
@@ -130,7 +134,7 @@ def tile_attend_vqattention_kernel(tc, query, book_words, book_scales, size, val
             out=weights[:],
             in0=probs[:],
             scalar=inv_sum[:],
-            in1=size_rows[:].rearrange("q c m -> q (c m)"),
+            in1=size_rows[:],
             op0=ALU.mult,
             op1=ALU.mult,
         )
@@ -177,7 +181,7 @@ def tile_attend_vqattention_kernel(tc, query, book_words, book_scales, size, val
         words = gathered3[:].bitcast(F32)
         turned = psum.tile([P, 2, P], F32, name="turned", tag="bank1")
         for u in range(2):
-            nc.tensor.transpose(turned[:, u, :], words[:, u : 2 * P : 2], ident[:])
+            nc.tensor.transpose(turned[:, u, :], words[:, u * P : (u + 1) * P], ident[:])
         halves = []
         for h in range(2):
             late = keep.tile([P, I // 2], BF16, name=f"late{h}", align_bytes=64)

@@ -61,11 +61,8 @@ def tile_attend_vqattention_kernel(tc, query, book_words, book_scales, size, val
             out=book_codes[:].bitcast(I32),
             in_=book_words[0].rearrange("p c t -> p (c t)").bitcast(I32),
         )
-        for quad in range(4):
-            nc.sync.dma_start(
-                out=book_plane[32 * quad : 32 * quad + 4, :].bitcast(I32),
-                in_=scale_rows[4 * quad : 4 * quad + 4, :],
-            )
+        for r in range(4):
+            nc.sync.dma_start(out=book_plane[r:P:32, :].bitcast(I32), in_=scale_rows[r:16:4, :])
         nc.sync.dma_start(code_list[:], offs)
         nc.sync.dma_start(out=pools[0][:], in_=vals[P : 2 * P, :])
         nc.sync.dma_start(out=size_chunks[:CHUNKS, :], in_=size[0].rearrange("(c m) -> c m", m=P))

@@ -19,6 +19,7 @@ ACT = mybir.ActivationFunctionType
 P = 128
 PACK = 4
 HALF = P // 2
+CAST_SPLIT = 1536
 CHUNKS = I // P
 POOL_BYTES = 4 * T
 
@@ -53,7 +54,7 @@ def tile_attend_vqattention_kernel(tc, query, book_words, book_scales, size, val
         pools = [shared.tile([P, T], F32, name=f"pool{j}", offset=j * POOL_BYTES) for j in range(E // P)]
         ident = keep.tile([P, P], F32, name="ident")
 
-        nc.gpsimd.memset(book_plane[:].bitcast(I32), 0)
+        nc.vector.memset(book_plane[:].bitcast(I32), 0)
         nc.gpsimd.memset(size_chunks[:], 0.0)
         scale_rows = book_scales[0].bitcast(I32)
         nc.sync.dma_start(out=q_raw[:], in_=query.rearrange("(p j) q -> p j q", j=PACK))
@@ -82,7 +83,13 @@ def tile_attend_vqattention_kernel(tc, query, book_words, book_scales, size, val
         nc.vector.quantize_mx(out=q_codes[:].bitcast(FP8X4), scales=q_plane[:], in_=q_grouped[:])
 
         scores = keep.tile([P, C], F32, name="scores")
-        pieces = ((0, 512, nc.scalar.copy), (512, 768, nc.vector.tensor_copy), (768, 1024, nc.scalar.copy))
+        pieces = (
+            (0, 256, nc.vector.tensor_copy),
+            (256, 512, nc.scalar.copy),
+            (512, 768, nc.vector.tensor_copy),
+            (768, 896, nc.scalar.copy),
+            (896, 1024, nc.vector.tensor_copy),
+        )
         for h, (first, last, copy_out) in enumerate(pieces):
             cols = slice(first, last)
             acc = psum.tile([P, last - first], F32, name="score_bank", tag=f"bank{h}")
@@ -97,7 +104,7 @@ def tile_attend_vqattention_kernel(tc, query, book_words, book_scales, size, val
             )
             copy_out(out=scores[:, cols], in_=acc[:])
 
-        size_turned = psum.tile([P, P], F32, name="size_turned", tag="bank3")
+        size_turned = psum.tile([P, P], F32, name="size_turned", tag="bank5")
         nc.tensor.transpose(size_turned[:], size_chunks[:], ident[:])
         size_col = keep.tile([P, CHUNKS], F32, name="size_col")
         nc.scalar.copy(out=size_col[:], in_=size_turned[:, :CHUNKS])
@@ -106,13 +113,14 @@ def tile_attend_vqattention_kernel(tc, query, book_words, book_scales, size, val
             nc.tensor.transpose(dealt(size_rows[:])[:, 4 * c : 4 * c + 4], size_col[:, c : c + 1].to_broadcast([P, P]), ident[:])
 
         pool0_bf16 = keep.tile([P, T], BF16, name="pool0_bf16", align_bytes=64)
-        nc.scalar.activation(out=pool0_bf16[:], in_=pools[0][:], func=ACT.Copy)
+        nc.scalar.activation(out=pool0_bf16[:, :CAST_SPLIT], in_=pools[0][:, :CAST_SPLIT], func=ACT.Copy)
 
         picked = keep.tile([P, I], F32, name="picked", tag="gathered0", align_bytes=64)
         neg_max = keep.tile([P, 1], F32, name="neg_max")
         probs = shared.tile([P, I], F32, name="probs", offset=0)
         row_sum = keep.tile([P, 1], F32, name="row_sum")
         nc.vector.tensor_copy(out=picked[:], in_=scores[:].indirect(code_list[:]))
+        nc.vector.tensor_copy(out=pool0_bf16[:, CAST_SPLIT:], in_=pools[0][:, CAST_SPLIT:])
         nc.vector.tensor_reduce(out=neg_max[:], in_=picked[:], axis=mybir.AxisListType.X, op=ALU.max, negate=True)
         nc.scalar.activation(out=dealt(probs[:]), in_=picked[:].rearrange("p (b u j) -> p b u j", u=2, j=16), func=ACT.Exp, bias=neg_max[:], accum_out=row_sum[:])
 
@@ -192,9 +200,9 @@ def tile_attend_vqattention_kernel(tc, query, book_words, book_scales, size, val
         multiply(out12[:], w1_mx, mid_mx, slice(0, 2 * P))
         store(out12, P, nc.scalar.copy)
         last = keep.tile([P, P], F32, name="last")
-        for h, copy_out in enumerate((nc.scalar.copy, nc.vector.tensor_copy)):
+        for h, copy_out in enumerate((nc.vector.tensor_copy, nc.scalar.copy)):
             late_mx = quantise(halves[h][:], f"late{h}", 4 * POOL_BYTES + 256 * h)
             late_out = psum.tile([P, HALF], F32, name=f"late_out{h}")
             multiply(late_out[:], w1_mx, late_mx, slice(0, HALF))
             copy_out(out=last[:, h * HALF : (h + 1) * HALF], in_=late_out[:])
-        nc.sync.dma_start(out=out[:, 3 * P :], in_=last[:])
+        nc.scalar.dma_start(out=out[:, 3 * P :], in_=last[:])

@@ -65,11 +65,10 @@ def tile_attend_vqattention_kernel(tc, query, book_words, book_scales, size, val
         for r in range(4):
             nc.sync.dma_start(out=book_plane[r:P:32, :].bitcast(I32), in_=scale_rows[r:16:4, :])
         nc.sync.dma_start(code_list[:], offs)
-        nc.sync.dma_start(out=pools[0][:], in_=vals[P : 2 * P, :])
-        nc.sync.dma_start(out=size_chunks[:CHUNKS, :], in_=size[0].rearrange("(c m) -> c m", m=P))
-        nc.sync.dma_start(out=pools[1][:], in_=vals[0:P, :])
+        nc.sync.dma_start(out=pools[0][:], in_=vals[0:P, :])
         nc.sync.dma_start(token_list[:], offs2)
-        for j in (2, 3):
+        nc.sync.dma_start(out=size_chunks[:CHUNKS, :], in_=size[0].rearrange("(c m) -> c m", m=P))
+        for j in (1, 2, 3):
             nc.sync.dma_start(out=pools[j][:], in_=vals[j * P : (j + 1) * P, :])
         make_identity(nc, ident[:])
 
@@ -82,7 +81,7 @@ def tile_attend_vqattention_kernel(tc, query, book_words, book_scales, size, val
         )
         nc.vector.quantize_mx(out=q_codes[:].bitcast(FP8X4), scales=q_plane[:], in_=q_grouped[:])
 
-        scores = keep.tile([P, C], F32, name="scores")
+        scores = keep.tile([P, C], F32, name="scores", align_bytes=64)
         pieces = (
             (0, 256, nc.vector.tensor_copy),
             (256, 512, nc.scalar.copy),
@@ -112,15 +111,13 @@ def tile_attend_vqattention_kernel(tc, query, book_words, book_scales, size, val
         for c in range(CHUNKS):
             nc.tensor.transpose(dealt(size_rows[:])[:, 4 * c : 4 * c + 4], size_col[:, c : c + 1].to_broadcast([P, P]), ident[:])
 
-        pool0_bf16 = keep.tile([P, T], BF16, name="pool0_bf16", align_bytes=64)
-        nc.scalar.activation(out=pool0_bf16[:, :CAST_SPLIT], in_=pools[0][:, :CAST_SPLIT], func=ACT.Copy)
-
-        picked = keep.tile([P, I], F32, name="picked", tag="gathered0", align_bytes=64)
+        picked = keep.tile([P, I], F32, name="picked")
         neg_max = keep.tile([P, 1], F32, name="neg_max")
-        probs = shared.tile([P, I], F32, name="probs", offset=0)
+        probs = keep.tile([P, I], F32, name="probs", tag="size_chunks")
         row_sum = keep.tile([P, 1], F32, name="row_sum")
+        inv_sum = keep.tile([P, 1], F32, name="inv_sum")
+        weights = keep.tile([P, I], BF16, name="weights", align_bytes=64)
         nc.vector.tensor_copy(out=picked[:], in_=scores[:].indirect(code_list[:]))
-        nc.vector.tensor_copy(out=pool0_bf16[:, CAST_SPLIT:], in_=pools[0][:, CAST_SPLIT:])
         nc.vector.tensor_reduce(out=neg_max[:], in_=picked[:], axis=mybir.AxisListType.X, op=ALU.max, negate=True)
         nc.scalar.activation(out=dealt(probs[:]), in_=picked[:].rearrange("p (b u j) -> p b u j", u=2, j=16), func=ACT.Exp, bias=neg_max[:], accum_out=row_sum[:])
 
@@ -128,12 +125,7 @@ def tile_attend_vqattention_kernel(tc, query, book_words, book_scales, size, val
             nc.vector.tensor_copy(out=dealt(picked_vals[:]), in_=pools[j][:].indirect(token_list[:]))
             return picked_vals
 
-        gathered0 = keep.tile([P, I], BF16, name="gathered0", align_bytes=64)
-        nc.scalar.activation(out=dealt(gathered0[:]), in_=pool0_bf16[:].indirect(token_list[:]), func=ACT.Copy)
-        gathered1 = gather(1, keep.tile([P, I], BF16, name="gathered1", align_bytes=64))
-        inv_sum = shared.tile([P, 1], F32, name="inv_sum", offset=POOL_BYTES)
-
-        weights = keep.tile([P, I], BF16, name="weights", align_bytes=64)
+        gathered0 = gather(0, keep.tile([P, I], BF16, name="gathered0", tag="scores", align_bytes=64))
         nc.vector.reciprocal(out=inv_sum[:], in_=row_sum[:])
         nc.vector.scalar_tensor_tensor(
             out=weights[:],
@@ -143,6 +135,10 @@ def tile_attend_vqattention_kernel(tc, query, book_words, book_scales, size, val
             op0=ALU.mult,
             op1=ALU.mult,
         )
+
+        pool1_bf16 = keep.tile([P, T], BF16, name="pool1_bf16", align_bytes=64)
+        nc.scalar.activation(out=pool1_bf16[:, :CAST_SPLIT], in_=pools[1][:, :CAST_SPLIT], func=ACT.Copy)
+        nc.vector.tensor_copy(out=pool1_bf16[:, CAST_SPLIT:], in_=pools[1][:, CAST_SPLIT:])
 
         def turn_rows(bank, rows, grouped):
             turned = psum.tile([P, 2, P], F32, name="turned", tag=bank)
@@ -172,13 +168,16 @@ def tile_attend_vqattention_kernel(tc, query, book_words, book_scales, size, val
             copy_out(out=result[:], in_=acc[:])
             nc.sync.dma_start(out=out[:, first : first + width], in_=result[:])
 
-        grouped = keep.tile([P, 4 * I], BF16, name="grouped", tag="pool0_bf16", align_bytes=64)
-        turn_rows("bank1", gathered1, grouped[:, I : 2 * I])
-        turn_rows("bank2", weights, grouped[:, :I])
-        turn_rows("bank0", gathered0, grouped[:, 2 * I : 3 * I])
+        early = shared.tile([P, 2 * I], BF16, name="early", offset=POOL_BYTES, align_bytes=64)
+        grouped = keep.tile([P, 2 * I], BF16, name="grouped", align_bytes=64)
+        turn_rows("bank5", gathered0, early[:, I:])
+        turn_rows("bank2", weights, early[:, :I])
+        gathered1 = keep.tile([P, I], BF16, name="gathered1", align_bytes=64)
+        nc.scalar.activation(out=dealt(gathered1[:]), in_=pool1_bf16[:].indirect(token_list[:]), func=ACT.Copy)
         gathered2 = gather(2, keep.tile([P, I], BF16, name="gathered2", align_bytes=64))
-        turn_rows("bank3", gathered2, grouped[:, 3 * I :])
-        w1_mx = quantise(grouped[:, : 2 * I], "w1", 2 * POOL_BYTES)
+        turn_rows("bank3", gathered2, grouped[:, I:])
+        turn_rows("bank0", gathered1, grouped[:, :I])
+        w1_mx = quantise(early[:], "w1", 2 * POOL_BYTES)
         out0 = psum.tile([P, P], F32, name="out0", tag="bank4")
         multiply(out0[:], w1_mx, w1_mx, slice(P, 2 * P))
         store(out0, 0, nc.scalar.copy)
@@ -195,7 +194,7 @@ def tile_attend_vqattention_kernel(tc, query, book_words, book_scales, size, val
                 in_=turned[:, :, h * HALF : (h + 1) * HALF].rearrange("p u r -> p r u"),
             )
             halves.append(late)
-        mid_mx = quantise(grouped[:, 2 * I :], "mid", 3 * POOL_BYTES)
+        mid_mx = quantise(grouped[:], "mid", 3 * POOL_BYTES)
         out12 = psum.tile([P, 2 * P], F32, name="out12", tag="bank5")
         multiply(out12[:], w1_mx, mid_mx, slice(0, 2 * P))
         store(out12, P, nc.scalar.copy)

@@ -177,7 +177,7 @@ def tile_attend_vqattention_kernel(tc, query, book_words, book_scales, size, val
         gathered2 = gather(2, keep.tile([P, I], BF16, name="gathered2", align_bytes=64))
         turn_rows("bank3", gathered2, grouped[:, I:])
         turn_rows("bank0", gathered1, grouped[:, :I])
-        w1_mx = quantise(early[:], "w1", 2 * POOL_BYTES)
+        w1_mx = quantise(early[:], "w1", 4 * POOL_BYTES + 1024)
         out0 = psum.tile([P, P], F32, name="out0", tag="bank4")
         multiply(out0[:], w1_mx, w1_mx, slice(P, 2 * P))
         store(out0, 0, nc.scalar.copy)

@@ -19,23 +19,10 @@ ACT = mybir.ActivationFunctionType
 P = 128
 PACK = 4
 HALF = P // 2
-CAST_SPLIT = 1536
 CHUNKS = I // P
+LIST_COLS = I // 16
+VECTOR_COLS = 20
 POOL_BYTES = 4 * T
-
-
-def dealt(rows):
-    return rows.rearrange("p (u b j) -> p b u j", u=2, j=16)
-
-
-def turn(nc, rows, ident, turned, grouped):
-    words = rows[:].bitcast(F32)
-    for u in range(2):
-        nc.tensor.transpose(turned[:, u, :], words[:, u * P : (u + 1) * P], ident[:])
-    nc.scalar.copy(
-        out=grouped.bitcast(F32).rearrange("p (r u) -> p r u", u=2),
-        in_=turned[:].rearrange("p u r -> p r u"),
-    )
 
 
 def tile_attend_vqattention_kernel(tc, query, book_words, book_scales, size, vals, offs, offs2, out):
@@ -45,8 +32,8 @@ def tile_attend_vqattention_kernel(tc, query, book_words, book_scales, size, val
         shared = ctx.enter_context(tc.tile_pool(name="shared", bufs=1))
         psum = ctx.enter_context(tc.psum_pool(name="psum", bufs=1))
 
-        code_list = keep.tile([P, I // 16], U16, name="code_list")
-        token_list = keep.tile([P, I // 16], U16, name="token_list")
+        code_list = keep.tile([P, LIST_COLS], U16, name="code_list")
+        token_list = keep.tile([P, LIST_COLS], U16, name="token_list")
         q_raw = keep.tile([P, PACK, Q], F32, name="q_raw")
         book_codes = keep.tile([P, C], U32, name="book_codes", align_bytes=64)
         book_plane = keep.tile([P, C], U8, name="book_plane", align_bytes=64)
@@ -109,23 +96,26 @@ def tile_attend_vqattention_kernel(tc, query, book_words, book_scales, size, val
         nc.scalar.copy(out=size_col[:], in_=size_turned[:, :CHUNKS])
         size_rows = psum.tile([P, I], F32, name="size_rows", tag="bank0")
         for c in range(CHUNKS):
-            nc.tensor.transpose(dealt(size_rows[:])[:, 4 * c : 4 * c + 4], size_col[:, c : c + 1].to_broadcast([P, P]), ident[:])
+            nc.tensor.transpose(size_rows[:, c * P : (c + 1) * P], size_col[:, c : c + 1].to_broadcast([P, P]), ident[:])
 
-        picked = keep.tile([P, I], F32, name="picked")
+        def gather(picked, window, slots, vector_cols):
+            cut = 16 * vector_cols
+            if vector_cols > 0:
+                nc.vector.tensor_copy(out=picked[:, :cut], in_=window[:].indirect(slots[:, :vector_cols]))
+            if vector_cols < LIST_COLS:
+                nc.scalar.activation(out=picked[:, cut:], in_=window[:].indirect(slots[:, vector_cols:]), func=ACT.Copy)
+            return picked
+
+        picked = gather(keep.tile([P, I], F32, name="picked"), scores, code_list, VECTOR_COLS)
         neg_max = keep.tile([P, 1], F32, name="neg_max")
         probs = keep.tile([P, I], F32, name="probs", tag="size_chunks")
         row_sum = keep.tile([P, 1], F32, name="row_sum")
         inv_sum = keep.tile([P, 1], F32, name="inv_sum")
         weights = keep.tile([P, I], BF16, name="weights", align_bytes=64)
-        nc.vector.tensor_copy(out=picked[:], in_=scores[:].indirect(code_list[:]))
         nc.vector.tensor_reduce(out=neg_max[:], in_=picked[:], axis=mybir.AxisListType.X, op=ALU.max, negate=True)
-        nc.scalar.activation(out=dealt(probs[:]), in_=picked[:].rearrange("p (b u j) -> p b u j", u=2, j=16), func=ACT.Exp, bias=neg_max[:], accum_out=row_sum[:])
+        nc.scalar.activation(out=probs[:], in_=picked[:], func=ACT.Exp, bias=neg_max[:], accum_out=row_sum[:])
 
-        def gather(j, picked_vals):
-            nc.vector.tensor_copy(out=dealt(picked_vals[:]), in_=pools[j][:].indirect(token_list[:]))
-            return picked_vals
-
-        gathered0 = gather(0, keep.tile([P, I], BF16, name="gathered0", tag="scores", align_bytes=64))
+        gathered0 = gather(keep.tile([P, I], BF16, name="gathered0", tag="scores", align_bytes=64), pools[0], token_list, VECTOR_COLS)
         nc.vector.reciprocal(out=inv_sum[:], in_=row_sum[:])
         nc.vector.scalar_tensor_tensor(
             out=weights[:],
@@ -135,14 +125,20 @@ def tile_attend_vqattention_kernel(tc, query, book_words, book_scales, size, val
             op0=ALU.mult,
             op1=ALU.mult,
         )
+        gathered1 = gather(keep.tile([P, I], BF16, name="gathered1", align_bytes=64), pools[1], token_list, 0)
 
-        pool1_bf16 = keep.tile([P, T], BF16, name="pool1_bf16", align_bytes=64)
-        nc.scalar.activation(out=pool1_bf16[:, :CAST_SPLIT], in_=pools[1][:, :CAST_SPLIT], func=ACT.Copy)
-        nc.vector.tensor_copy(out=pool1_bf16[:, CAST_SPLIT:], in_=pools[1][:, CAST_SPLIT:])
-
-        def turn_rows(bank, rows, grouped):
+        def turn(bank, rows):
             turned = psum.tile([P, 2, P], F32, name="turned", tag=bank)
-            turn(nc, rows, ident, turned, grouped)
+            words = rows[:].bitcast(F32)
+            for u in range(2):
+                nc.tensor.transpose(turned[:, u, :], words[:, u : 2 * P : 2], ident[:])
+            return turned
+
+        def weave(grouped, turned, copy_out):
+            copy_out(
+                out=grouped.bitcast(F32).rearrange("p (r u) -> p r u", u=2),
+                in_=turned.rearrange("p u r -> p r u"),
+            )
 
         def quantise(grouped, name, offset):
             width = grouped.shape[1] // PACK
@@ -168,40 +164,35 @@ def tile_attend_vqattention_kernel(tc, query, book_words, book_scales, size, val
             copy_out(out=result[:], in_=acc[:])
             nc.sync.dma_start(out=out[:, first : first + width], in_=result[:])
 
-        early = shared.tile([P, 2 * I], BF16, name="early", offset=POOL_BYTES, align_bytes=64)
-        grouped = keep.tile([P, 2 * I], BF16, name="grouped", align_bytes=64)
-        turn_rows("bank5", gathered0, early[:, I:])
-        turn_rows("bank2", weights, early[:, :I])
-        gathered1 = keep.tile([P, I], BF16, name="gathered1", align_bytes=64)
-        nc.scalar.activation(out=dealt(gathered1[:]), in_=pool1_bf16[:].indirect(token_list[:]), func=ACT.Copy)
-        gathered2 = gather(2, keep.tile([P, I], BF16, name="gathered2", align_bytes=64))
-        turn_rows("bank3", gathered2, grouped[:, I:])
-        turn_rows("bank0", gathered1, grouped[:, :I])
-        w1_mx = quantise(early[:], "w1", 4 * POOL_BYTES + 1024)
-        out0 = psum.tile([P, P], F32, name="out0", tag="bank4")
-        multiply(out0[:], w1_mx, w1_mx, slice(P, 2 * P))
-        store(out0, 0, nc.scalar.copy)
-        gathered3 = gather(3, shared.tile([P, I], BF16, name="gathered3", offset=0))
-        words = gathered3[:].bitcast(F32)
-        turned = psum.tile([P, 2, P], F32, name="turned", tag="bank1")
-        for u in range(2):
-            nc.tensor.transpose(turned[:, u, :], words[:, u * P : (u + 1) * P], ident[:])
+        early = keep.tile([P, 3 * I], BF16, name="early", align_bytes=64)
+        weave(early[:, I : 2 * I], turn("bank5", gathered0)[:], nc.vector.tensor_copy)
+        weave(early[:, :I], turn("bank2", weights)[:], nc.vector.tensor_copy)
+        weave(early[:, 2 * I :], turn("bank3", gathered1)[:], nc.scalar.copy)
+        gathered2 = gather(keep.tile([P, I], BF16, name="gathered2", align_bytes=64), pools[2], token_list, VECTOR_COLS)
+        turned2 = turn("bank1", gathered2)
+        early_mx = quantise(early[:], "early", 2 * POOL_BYTES)
+        out01 = psum.tile([P, 2 * P], F32, name="out01", tag="bank4")
+        multiply(out01[:], early_mx, early_mx, slice(P, 3 * P))
+        gathered3 = gather(keep.tile([P, I], BF16, name="gathered3", align_bytes=64), pools[3], token_list, VECTOR_COLS)
+        turned3 = turn("bank0", gathered3)
+        middle = shared.tile([P, I], BF16, name="middle", offset=3 * POOL_BYTES, align_bytes=64)
+        weave(middle[:], turned2[:], nc.scalar.copy)
+        result01 = shared.tile([P, 2 * P], F32, name="result01", offset=3 * POOL_BYTES + 1024)
+        nc.vector.tensor_copy(out=result01[:], in_=out01[:])
+        nc.sync.dma_start(out=out[:, : 2 * P], in_=result01[:])
+        mid_mx = quantise(middle[:], "mid", 4 * POOL_BYTES)
         halves = []
         for h in range(2):
             late = keep.tile([P, I // 2], BF16, name=f"late{h}", align_bytes=64)
-            nc.scalar.copy(
-                out=late[:].bitcast(F32).rearrange("p (r u) -> p r u", u=2),
-                in_=turned[:, :, h * HALF : (h + 1) * HALF].rearrange("p u r -> p r u"),
-            )
+            weave(late[:], turned3[:, :, h * HALF : (h + 1) * HALF], nc.scalar.copy)
             halves.append(late)
-        mid_mx = quantise(grouped[:], "mid", 3 * POOL_BYTES)
-        out12 = psum.tile([P, 2 * P], F32, name="out12", tag="bank5")
-        multiply(out12[:], w1_mx, mid_mx, slice(0, 2 * P))
-        store(out12, P, nc.scalar.copy)
+        out2 = psum.tile([P, P], F32, name="out2", tag="bank5")
+        multiply(out2[:], early_mx, mid_mx, slice(0, P))
+        store(out2, 2 * P, nc.scalar.copy)
         last = keep.tile([P, P], F32, name="last")
         for h, copy_out in enumerate((nc.vector.tensor_copy, nc.scalar.copy)):
-            late_mx = quantise(halves[h][:], f"late{h}", 4 * POOL_BYTES + 256 * h)
+            late_mx = quantise(halves[h][:], f"late{h}", 4 * POOL_BYTES + 2048 + 256 * h)
             late_out = psum.tile([P, HALF], F32, name=f"late_out{h}")
-            multiply(late_out[:], w1_mx, late_mx, slice(0, HALF))
+            multiply(late_out[:], early_mx, late_mx, slice(0, HALF))
             copy_out(out=last[:, h * HALF : (h + 1) * HALF], in_=late_out[:])
         nc.scalar.dma_start(out=out[:, 3 * P :], in_=last[:])

@@ -21,7 +21,8 @@ PACK = 4
 HALF = P // 2
 CHUNKS = I // P
 LIST_COLS = I // 16
-VECTOR_COLS = 20
+VECTOR_COLS = 16
+LAST_COLS = 16
 POOL_BYTES = 4 * T
 
 
@@ -164,16 +165,22 @@ def tile_attend_vqattention_kernel(tc, query, book_words, book_scales, size, val
             copy_out(out=result[:], in_=acc[:])
             nc.sync.dma_start(out=out[:, first : first + width], in_=result[:])
 
-        early = keep.tile([P, 3 * I], BF16, name="early", align_bytes=64)
-        weave(early[:, I : 2 * I], turn("bank5", gathered0)[:], nc.vector.tensor_copy)
-        weave(early[:, :I], turn("bank2", weights)[:], nc.vector.tensor_copy)
-        weave(early[:, 2 * I :], turn("bank3", gathered1)[:], nc.scalar.copy)
-        gathered2 = gather(keep.tile([P, I], BF16, name="gathered2", align_bytes=64), pools[2], token_list, VECTOR_COLS)
+        early = keep.tile([P, 2 * I], BF16, name="early", align_bytes=64)
+        weave(early[:, I:], turn("bank5", gathered0)[:], nc.vector.tensor_copy)
+        weave(early[:, :I], turn("bank2", weights)[:], nc.scalar.copy)
+        turned1 = turn("bank3", gathered1)
+        gathered2 = gather(keep.tile([P, I], BF16, name="gathered2", align_bytes=64), pools[2], token_list, 20)
         turned2 = turn("bank1", gathered2)
-        early_mx = quantise(early[:], "early", 2 * POOL_BYTES)
+        second = shared.tile([P, I], BF16, name="second", offset=2 * POOL_BYTES, align_bytes=64)
+        early_codes = shared.tile([P, 3 * P], U32, name="early_codes", offset=2 * POOL_BYTES + 1024, align_bytes=64)
+        early_plane = keep.tile([P, 3 * P], U8, name="early_plane", align_bytes=64)
+        early_mx = early_codes, early_plane
+        weave(second[:], turned1[:], nc.scalar.copy)
+        nc.vector.quantize_mx(out=early_codes[:, : 2 * P].bitcast(FP8X4), scales=early_plane[:, : 2 * P], in_=early[:])
+        nc.vector.quantize_mx(out=early_codes[:, 2 * P :].bitcast(FP8X4), scales=early_plane[:, 2 * P :], in_=second[:])
         out01 = psum.tile([P, 2 * P], F32, name="out01", tag="bank4")
         multiply(out01[:], early_mx, early_mx, slice(P, 3 * P))
-        gathered3 = gather(keep.tile([P, I], BF16, name="gathered3", align_bytes=64), pools[3], token_list, VECTOR_COLS)
+        gathered3 = gather(keep.tile([P, I], BF16, name="gathered3", align_bytes=64), pools[3], token_list, LAST_COLS)
         turned3 = turn("bank0", gathered3)
         middle = shared.tile([P, I], BF16, name="middle", offset=3 * POOL_BYTES, align_bytes=64)
         weave(middle[:], turned2[:], nc.scalar.copy)

@@ -23,6 +23,7 @@ CHUNKS = I // P
 LIST_COLS = I // 16
 VECTOR_COLS = 16
 LAST_COLS = 16
+SIZE_ROWS = slice(8, P, 36)
 POOL_BYTES = 4 * T
 
 
@@ -55,7 +56,7 @@ def tile_attend_vqattention_kernel(tc, query, book_words, book_scales, size, val
         nc.sync.dma_start(code_list[:], offs)
         nc.sync.dma_start(out=pools[0][:], in_=vals[0:P, :])
         nc.sync.dma_start(token_list[:], offs2)
-        nc.sync.dma_start(out=size_chunks[:CHUNKS, :], in_=size[0].rearrange("(c m) -> c m", m=P))
+        nc.sync.dma_start(out=size_chunks[SIZE_ROWS, :], in_=size[0].rearrange("(c m) -> c m", m=P))
         for j in (1, 2, 3):
             nc.sync.dma_start(out=pools[j][:], in_=vals[j * P : (j + 1) * P, :])
         make_identity(nc, ident[:])
@@ -94,7 +95,7 @@ def tile_attend_vqattention_kernel(tc, query, book_words, book_scales, size, val
         size_turned = psum.tile([P, P], F32, name="size_turned", tag="bank5")
         nc.tensor.transpose(size_turned[:], size_chunks[:], ident[:])
         size_col = keep.tile([P, CHUNKS], F32, name="size_col")
-        nc.scalar.copy(out=size_col[:], in_=size_turned[:, :CHUNKS])
+        nc.scalar.copy(out=size_col[:], in_=size_turned[:, SIZE_ROWS])
         size_rows = psum.tile([P, I], F32, name="size_rows", tag="bank0")
         for c in range(CHUNKS):
             nc.tensor.transpose(size_rows[:, c * P : (c + 1) * P], size_col[:, c : c + 1].to_broadcast([P, P]), ident[:])
@@ -197,7 +198,7 @@ def tile_attend_vqattention_kernel(tc, query, book_words, book_scales, size, val
         multiply(out2[:], early_mx, mid_mx, slice(0, P))
         store(out2, 2 * P, nc.scalar.copy)
         last = keep.tile([P, P], F32, name="last")
-        for h, copy_out in enumerate((nc.vector.tensor_copy, nc.scalar.copy)):
+        for h, copy_out in enumerate((nc.scalar.copy, nc.scalar.copy)):
             late_mx = quantise(halves[h][:], f"late{h}", 4 * POOL_BYTES + 2048 + 256 * h)
             late_out = psum.tile([P, HALF], F32, name=f"late_out{h}")
             multiply(late_out[:], early_mx, late_mx, slice(0, HALF))

@@ -203,4 +203,4 @@ def tile_attend_vqattention_kernel(tc, query, book_words, book_scales, size, val
             late_out = psum.tile([P, HALF], F32, name=f"late_out{h}")
             multiply(late_out[:], early_mx, late_mx, slice(0, HALF))
             copy_out(out=last[:, h * HALF : (h + 1) * HALF], in_=late_out[:])
-        nc.scalar.dma_start(out=out[:, 3 * P :], in_=last[:])
+        nc.sync.dma_start(out=out[:, 3 * P :], in_=last[:])

@@ -21,8 +21,9 @@ PACK = 4
 HALF = P // 2
 CHUNKS = I // P
 LIST_COLS = I // 16
-VECTOR_COLS = 16
-LAST_COLS = 16
+SHARE = 16
+NARROW_ROWS = slice(32, 96)
+EARLY = 2 * P + HALF
 SIZE_ROWS = slice(8, P, 36)
 POOL_BYTES = 4 * T
 
@@ -39,11 +40,15 @@ def tile_attend_vqattention_kernel(tc, query, book_words, book_scales, size, val
         q_raw = keep.tile([P, PACK, Q], F32, name="q_raw")
         book_codes = keep.tile([P, C], U32, name="book_codes", align_bytes=64)
         book_plane = keep.tile([P, C], U8, name="book_plane", align_bytes=64)
-        size_chunks = keep.tile([P, P], F32, name="size_chunks")
-        pools = [shared.tile([P, T], F32, name=f"pool{j}", offset=j * POOL_BYTES) for j in range(E // P)]
+        size_chunks = shared.tile([P, P], F32, name="size_chunks", offset=4 * POOL_BYTES + 768)
+        first = shared.tile([P, T], F32, name="first", offset=0)
+        narrow = shared.tile([P, T], F32, name="narrow", offset=POOL_BYTES)
+        third = shared.tile([P, T], F32, name="third", offset=2 * POOL_BYTES)
+        fourth = shared.tile([P, T], F32, name="fourth", offset=3 * POOL_BYTES)
         ident = keep.tile([P, P], F32, name="ident")
 
         nc.vector.memset(book_plane[:].bitcast(I32), 0)
+        nc.vector.memset(narrow[:].bitcast(I32), 0)
         nc.gpsimd.memset(size_chunks[:], 0.0)
         scale_rows = book_scales[0].bitcast(I32)
         nc.sync.dma_start(out=q_raw[:], in_=query.rearrange("(p j) q -> p j q", j=PACK))
@@ -54,12 +59,15 @@ def tile_attend_vqattention_kernel(tc, query, book_words, book_scales, size, val
         for r in range(4):
             nc.sync.dma_start(out=book_plane[r:P:32, :].bitcast(I32), in_=scale_rows[r:16:4, :])
         nc.sync.dma_start(code_list[:], offs)
-        nc.sync.dma_start(out=pools[0][:], in_=vals[0:P, :])
+        nc.sync.dma_start(out=first[:], in_=vals[0:P, :])
         nc.sync.dma_start(token_list[:], offs2)
         nc.sync.dma_start(out=size_chunks[SIZE_ROWS, :], in_=size[0].rearrange("(c m) -> c m", m=P))
-        for j in (1, 2, 3):
-            nc.sync.dma_start(out=pools[j][:], in_=vals[j * P : (j + 1) * P, :])
+        nc.sync.dma_start(out=narrow[NARROW_ROWS, :], in_=vals[2 * P : EARLY, :])
+        nc.sync.dma_start(out=third[:], in_=vals[P : 2 * P, :])
+        nc.sync.dma_start(out=fourth[:], in_=vals[EARLY : EARLY + P, :])
         make_identity(nc, ident[:])
+        minus_one = keep.tile([P, 1], F32, name="minus_one")
+        nc.gpsimd.memset(minus_one[:], -1.0)
 
         q_grouped = keep.tile([P, Q * PACK], BF16, name="q_grouped", align_bytes=64)
         q_codes = keep.tile([P, Q], U32, name="q_codes", align_bytes=64)
@@ -78,9 +86,9 @@ def tile_attend_vqattention_kernel(tc, query, book_words, book_scales, size, val
             (768, 896, nc.scalar.copy),
             (896, 1024, nc.vector.tensor_copy),
         )
-        for h, (first, last, copy_out) in enumerate(pieces):
-            cols = slice(first, last)
-            acc = psum.tile([P, last - first], F32, name="score_bank", tag=f"bank{h}")
+        for h, (start, stop, copy_out) in enumerate(pieces):
+            cols = slice(start, stop)
+            acc = psum.tile([P, stop - start], F32, name="score_bank", tag=f"bank{h}")
             nc.tensor.matmul_mx(
                 out=acc[:],
                 lhsT=q_codes[:].bitcast(FP8X4),
@@ -94,11 +102,6 @@ def tile_attend_vqattention_kernel(tc, query, book_words, book_scales, size, val
 
         size_turned = psum.tile([P, P], F32, name="size_turned", tag="bank5")
         nc.tensor.transpose(size_turned[:], size_chunks[:], ident[:])
-        size_col = keep.tile([P, CHUNKS], F32, name="size_col")
-        nc.scalar.copy(out=size_col[:], in_=size_turned[:, SIZE_ROWS])
-        size_rows = psum.tile([P, I], F32, name="size_rows", tag="bank0")
-        for c in range(CHUNKS):
-            nc.tensor.transpose(size_rows[:, c * P : (c + 1) * P], size_col[:, c : c + 1].to_broadcast([P, P]), ident[:])
 
         def gather(picked, window, slots, vector_cols):
             cut = 16 * vector_cols
@@ -107,27 +110,6 @@ def tile_attend_vqattention_kernel(tc, query, book_words, book_scales, size, val
             if vector_cols < LIST_COLS:
                 nc.scalar.activation(out=picked[:, cut:], in_=window[:].indirect(slots[:, vector_cols:]), func=ACT.Copy)
             return picked
-
-        picked = gather(keep.tile([P, I], F32, name="picked"), scores, code_list, VECTOR_COLS)
-        neg_max = keep.tile([P, 1], F32, name="neg_max")
-        probs = keep.tile([P, I], F32, name="probs", tag="size_chunks")
-        row_sum = keep.tile([P, 1], F32, name="row_sum")
-        inv_sum = keep.tile([P, 1], F32, name="inv_sum")
-        weights = keep.tile([P, I], BF16, name="weights", align_bytes=64)
-        nc.vector.tensor_reduce(out=neg_max[:], in_=picked[:], axis=mybir.AxisListType.X, op=ALU.max, negate=True)
-        nc.scalar.activation(out=probs[:], in_=picked[:], func=ACT.Exp, bias=neg_max[:], accum_out=row_sum[:])
-
-        gathered0 = gather(keep.tile([P, I], BF16, name="gathered0", tag="scores", align_bytes=64), pools[0], token_list, VECTOR_COLS)
-        nc.vector.reciprocal(out=inv_sum[:], in_=row_sum[:])
-        nc.vector.scalar_tensor_tensor(
-            out=weights[:],
-            in0=probs[:],
-            scalar=inv_sum[:],
-            in1=size_rows[:],
-            op0=ALU.mult,
-            op1=ALU.mult,
-        )
-        gathered1 = gather(keep.tile([P, I], BF16, name="gathered1", align_bytes=64), pools[1], token_list, 0)
 
         def turn(bank, rows):
             turned = psum.tile([P, 2, P], F32, name="turned", tag=bank)
@@ -142,65 +124,93 @@ def tile_attend_vqattention_kernel(tc, query, book_words, book_scales, size, val
                 in_=turned.rearrange("p u r -> p r u"),
             )
 
-        def quantise(grouped, name, offset):
-            width = grouped.shape[1] // PACK
-            codes = shared.tile([P, width], U32, name=f"{name}_codes", offset=offset, align_bytes=64)
-            plane = keep.tile([P, width], U8, name=f"{name}_plane", align_bytes=64)
-            nc.vector.quantize_mx(out=codes[:].bitcast(FP8X4), scales=plane[:], in_=grouped)
-            return codes, plane
+        codes = shared.tile([P, Q + E], U32, name="codes", offset=2 * POOL_BYTES, align_bytes=64)
+        plane = keep.tile([P, Q + E], U8, name="plane", align_bytes=64)
 
-        def multiply(acc, w_mx, v_mx, cols):
+        def quantise(grouped, column):
+            cols = slice(column, column + grouped.shape[1] // PACK)
+            nc.vector.quantize_mx(out=codes[:, cols].bitcast(FP8X4), scales=plane[:, cols], in_=grouped)
+
+        def multiply(acc, feature):
+            cols = slice(Q + feature, Q + feature + acc.shape[1])
             nc.tensor.matmul_mx(
                 out=acc,
-                lhsT=w_mx[0][:, :Q].bitcast(FP8X4),
-                lhsT_scale=w_mx[1][:, :Q],
-                rhs=v_mx[0][:, cols].bitcast(FP8X4),
-                rhs_scale=v_mx[1][:, cols],
+                lhsT=codes[:, :Q].bitcast(FP8X4),
+                lhsT_scale=plane[:, :Q],
+                rhs=codes[:, cols].bitcast(FP8X4),
+                rhs_scale=plane[:, cols],
                 start=True,
                 stop=True,
             )
 
-        def store(acc, first, copy_out):
+        def store(acc, feature, copy_out):
             width = acc.shape[1]
-            result = keep.tile([P, width], F32, name=f"result{first}")
+            result = keep.tile([P, width], F32, name=f"result{feature}")
             copy_out(out=result[:], in_=acc[:])
-            nc.sync.dma_start(out=out[:, first : first + width], in_=result[:])
+            nc.sync.dma_start(out=out[:, feature : feature + width], in_=result[:])
 
-        early = keep.tile([P, 2 * I], BF16, name="early", align_bytes=64)
-        weave(early[:, I:], turn("bank5", gathered0)[:], nc.vector.tensor_copy)
-        weave(early[:, :I], turn("bank2", weights)[:], nc.scalar.copy)
-        turned1 = turn("bank3", gathered1)
-        gathered2 = gather(keep.tile([P, I], BF16, name="gathered2", align_bytes=64), pools[2], token_list, 20)
-        turned2 = turn("bank1", gathered2)
-        second = shared.tile([P, I], BF16, name="second", offset=2 * POOL_BYTES, align_bytes=64)
-        early_codes = shared.tile([P, 3 * P], U32, name="early_codes", offset=2 * POOL_BYTES + 1024, align_bytes=64)
-        early_plane = keep.tile([P, 3 * P], U8, name="early_plane", align_bytes=64)
-        early_mx = early_codes, early_plane
-        weave(second[:], turned1[:], nc.scalar.copy)
-        nc.vector.quantize_mx(out=early_codes[:, : 2 * P].bitcast(FP8X4), scales=early_plane[:, : 2 * P], in_=early[:])
-        nc.vector.quantize_mx(out=early_codes[:, 2 * P :].bitcast(FP8X4), scales=early_plane[:, 2 * P :], in_=second[:])
-        out01 = psum.tile([P, 2 * P], F32, name="out01", tag="bank4")
-        multiply(out01[:], early_mx, early_mx, slice(P, 3 * P))
-        gathered3 = gather(keep.tile([P, I], BF16, name="gathered3", align_bytes=64), pools[3], token_list, LAST_COLS)
-        turned3 = turn("bank0", gathered3)
-        middle = shared.tile([P, I], BF16, name="middle", offset=3 * POOL_BYTES, align_bytes=64)
-        weave(middle[:], turned2[:], nc.scalar.copy)
-        result01 = shared.tile([P, 2 * P], F32, name="result01", offset=3 * POOL_BYTES + 1024)
-        nc.vector.tensor_copy(out=result01[:], in_=out01[:])
-        nc.sync.dma_start(out=out[:, : 2 * P], in_=result01[:])
-        mid_mx = quantise(middle[:], "mid", 4 * POOL_BYTES)
-        halves = []
-        for h in range(2):
-            late = keep.tile([P, I // 2], BF16, name=f"late{h}", align_bytes=64)
-            weave(late[:], turned3[:, :, h * HALF : (h + 1) * HALF], nc.scalar.copy)
-            halves.append(late)
-        out2 = psum.tile([P, P], F32, name="out2", tag="bank5")
-        multiply(out2[:], early_mx, mid_mx, slice(0, P))
-        store(out2, 2 * P, nc.scalar.copy)
-        last = keep.tile([P, P], F32, name="last")
-        for h, copy_out in enumerate((nc.scalar.copy, nc.scalar.copy)):
-            late_mx = quantise(halves[h][:], f"late{h}", 4 * POOL_BYTES + 2048 + 256 * h)
-            late_out = psum.tile([P, HALF], F32, name=f"late_out{h}")
-            multiply(late_out[:], early_mx, late_mx, slice(0, HALF))
-            copy_out(out=last[:, h * HALF : (h + 1) * HALF], in_=late_out[:])
-        nc.sync.dma_start(out=out[:, 3 * P :], in_=last[:])
+        picked = gather(keep.tile([P, I], F32, name="picked"), scores, code_list, 20)
+        neg_max = keep.tile([P, 1], F32, name="neg_max")
+        probs = shared.tile([P, I], F32, name="probs", offset=4 * POOL_BYTES + 1024)
+        row_sum = keep.tile([P, 1], F32, name="row_sum")
+        inv_sum = keep.tile([P, 1], F32, name="inv_sum")
+        weights = shared.tile([P, I], BF16, name="weights", offset=POOL_BYTES)
+        nc.vector.tensor_reduce(out=neg_max[:], in_=picked[:], axis=mybir.AxisListType.X, op=ALU.max, negate=True)
+        gathered1 = gather(keep.tile([P, I], BF16, name="gathered1"), first, token_list, 0)
+        nc.sync.dma_start(out=first[NARROW_ROWS, :], in_=vals[E - HALF :, :])
+        size_col = keep.tile([P, CHUNKS], F32, name="size_col")
+        nc.scalar.copy(out=size_col[:], in_=size_turned[:, SIZE_ROWS])
+        nc.scalar.activation(out=probs[:], in_=picked[:], func=ACT.Exp, bias=neg_max[:], accum_out=row_sum[:])
+        size_rows = psum.tile([P, I], F32, name="size_rows", tag="bank0")
+        for c in range(CHUNKS):
+            nc.tensor.transpose(size_rows[:, c * P : (c + 1) * P], size_col[:, c : c + 1].to_broadcast([P, P]), ident[:])
+        turned1 = turn("bank5", gathered1)
+        gathered2 = gather(keep.tile([P, I], BF16, name="gathered2"), narrow, token_list, LIST_COLS)
+        nc.gpsimd.tensor_tensor(out=inv_sum[:], in0=row_sum[:], in1=minus_one[:], op=ALU.pow)
+        nc.vector.scalar_tensor_tensor(
+            out=weights[:],
+            in0=probs[:],
+            scalar=inv_sum[:],
+            in1=size_rows[:],
+            op0=ALU.mult,
+            op1=ALU.mult,
+        )
+
+        turned2 = turn("bank3", gathered2)
+        turned_w = turn("bank2", weights)
+        gathered3 = gather(keep.tile([P, I], BF16, name="gathered3"), third, token_list, 8)
+        turned3 = turn("bank1", gathered3)
+        grouped1 = shared.tile([P, I], BF16, name="grouped1", offset=2 * POOL_BYTES + 4096, align_bytes=64)
+        grouped_w = shared.tile([P, I], BF16, name="grouped_w", offset=2 * POOL_BYTES + 5120, align_bytes=64)
+        grouped2 = shared.tile([P, I // 2], BF16, name="grouped2", offset=2 * POOL_BYTES + 6144, align_bytes=64)
+        weave(grouped1[:], turned1[:], nc.vector.tensor_copy)
+        weave(grouped2[:], turned2[:, :, NARROW_ROWS], nc.vector.tensor_copy)
+        weave(grouped_w[:], turned_w[:], nc.scalar.copy)
+        quantise(grouped1[:], Q)
+        quantise(grouped_w[:], 0)
+        quantise(grouped2[:], Q + 2 * P)
+        grouped3 = keep.tile([P, I], BF16, name="grouped3", align_bytes=64)
+        weave(grouped3[:], turned3[:], nc.scalar.copy)
+        quantise(grouped3[:], Q + P)
+        early_out = psum.tile([P, EARLY], F32, name="early_out", tag="bank4")
+        multiply(early_out[:, : 2 * P], 0)
+        multiply(early_out[:, 2 * P :], 2 * P)
+        gathered4 = gather(keep.tile([P, I], BF16, name="gathered4", align_bytes=64), fourth, token_list, 12)
+        turned4 = turn("bank3", gathered4)
+        gathered5 = gather(keep.tile([P, I], BF16, name="gathered5", align_bytes=64), first, token_list, SHARE)
+        turned5 = turn("bank0", gathered5)
+        grouped4 = shared.tile([P, I], BF16, name="grouped4", offset=0, align_bytes=64)
+        weave(grouped4[:], turned4[:], nc.scalar.copy)
+        early_result = shared.tile([P, EARLY], F32, name="early_result", offset=1024)
+        nc.vector.tensor_copy(out=early_result[:], in_=early_out[:])
+        nc.sync.dma_start(out=out[:, :EARLY], in_=early_result[:])
+        quantise(grouped4[:], Q + EARLY)
+        grouped5 = keep.tile([P, I // 2], BF16, name="grouped5", align_bytes=64)
+        weave(grouped5[:], turned5[:, :, NARROW_ROWS], nc.scalar.copy)
+        out4 = psum.tile([P, P], F32, name="out4", tag="bank5")
+        multiply(out4[:], EARLY)
+        quantise(grouped5[:], Q + E - HALF)
+        store(out4, EARLY, nc.vector.tensor_copy)
+        out5 = psum.tile([P, HALF], F32, name="out5")
+        multiply(out5[:], E - HALF)
+        store(out5, E - HALF, nc.scalar.copy)

@@ -61,13 +61,11 @@ def tile_attend_vqattention_kernel(tc, query, book_words, book_scales, size, val
         nc.sync.dma_start(code_list[:], offs)
         nc.sync.dma_start(out=first[:], in_=vals[0:P, :])
         nc.sync.dma_start(token_list[:], offs2)
-        nc.sync.dma_start(out=size_chunks[SIZE_ROWS, :], in_=size[0].rearrange("(c m) -> c m", m=P))
         nc.sync.dma_start(out=narrow[NARROW_ROWS, :], in_=vals[2 * P : EARLY, :])
+        nc.sync.dma_start(out=size_chunks[SIZE_ROWS, :], in_=size[0].rearrange("(c m) -> c m", m=P))
         nc.sync.dma_start(out=third[:], in_=vals[P : 2 * P, :])
         nc.sync.dma_start(out=fourth[:], in_=vals[EARLY : EARLY + P, :])
         make_identity(nc, ident[:])
-        minus_one = keep.tile([P, 1], F32, name="minus_one")
-        nc.gpsimd.memset(minus_one[:], -1.0)
 
         q_grouped = keep.tile([P, Q * PACK], BF16, name="q_grouped", align_bytes=64)
         q_codes = keep.tile([P, Q], U32, name="q_codes", align_bytes=64)
@@ -112,7 +110,9 @@ def tile_attend_vqattention_kernel(tc, query, book_words, book_scales, size, val
             return picked
 
         def turn(bank, rows):
-            turned = psum.tile([P, 2, P], F32, name="turned", tag=bank)
+            return turn_into(psum.tile([P, 2, P], F32, name="turned", tag=bank), rows)
+
+        def turn_into(turned, rows):
             words = rows[:].bitcast(F32)
             for u in range(2):
                 nc.tensor.transpose(turned[:, u, :], words[:, u : 2 * P : 2], ident[:])
@@ -153,8 +153,8 @@ def tile_attend_vqattention_kernel(tc, query, book_words, book_scales, size, val
         neg_max = keep.tile([P, 1], F32, name="neg_max")
         probs = shared.tile([P, I], F32, name="probs", offset=4 * POOL_BYTES + 1024)
         row_sum = keep.tile([P, 1], F32, name="row_sum")
-        inv_sum = keep.tile([P, 1], F32, name="inv_sum")
-        weights = shared.tile([P, I], BF16, name="weights", offset=POOL_BYTES)
+        inv_sum = shared.tile([P, 1], F32, name="inv_sum", offset=4 * POOL_BYTES + 768)
+        weights = keep.tile([P, I], BF16, name="weights")
         nc.vector.tensor_reduce(out=neg_max[:], in_=picked[:], axis=mybir.AxisListType.X, op=ALU.max, negate=True)
         gathered1 = gather(keep.tile([P, I], BF16, name="gathered1"), first, token_list, 0)
         nc.sync.dma_start(out=first[NARROW_ROWS, :], in_=vals[E - HALF :, :])
@@ -164,9 +164,10 @@ def tile_attend_vqattention_kernel(tc, query, book_words, book_scales, size, val
         size_rows = psum.tile([P, I], F32, name="size_rows", tag="bank0")
         for c in range(CHUNKS):
             nc.tensor.transpose(size_rows[:, c * P : (c + 1) * P], size_col[:, c : c + 1].to_broadcast([P, P]), ident[:])
-        turned1 = turn("bank5", gathered1)
+        both = psum.tile([P, 4, P], F32, name="both", tag="bank5")
+        turned1 = turn_into(both[:, :2, :], gathered1)
         gathered2 = gather(keep.tile([P, I], BF16, name="gathered2"), narrow, token_list, LIST_COLS)
-        nc.gpsimd.tensor_tensor(out=inv_sum[:], in0=row_sum[:], in1=minus_one[:], op=ALU.pow)
+        nc.vector.reciprocal(out=inv_sum[:], in_=row_sum[:])
         nc.vector.scalar_tensor_tensor(
             out=weights[:],
             in0=probs[:],
@@ -176,18 +177,16 @@ def tile_attend_vqattention_kernel(tc, query, book_words, book_scales, size, val
             op1=ALU.mult,
         )
 
-        turned2 = turn("bank3", gathered2)
+        turned2 = turn_into(both[:, 2:, :], gathered2)
         turned_w = turn("bank2", weights)
         gathered3 = gather(keep.tile([P, I], BF16, name="gathered3"), third, token_list, 8)
         turned3 = turn("bank1", gathered3)
-        grouped1 = shared.tile([P, I], BF16, name="grouped1", offset=2 * POOL_BYTES + 4096, align_bytes=64)
-        grouped_w = shared.tile([P, I], BF16, name="grouped_w", offset=2 * POOL_BYTES + 5120, align_bytes=64)
+        grouped_w1 = shared.tile([P, 2 * I], BF16, name="grouped_w1", offset=2 * POOL_BYTES + 4096, align_bytes=64)
         grouped2 = shared.tile([P, I // 2], BF16, name="grouped2", offset=2 * POOL_BYTES + 6144, align_bytes=64)
-        weave(grouped1[:], turned1[:], nc.vector.tensor_copy)
+        weave(grouped_w1[:, I:], turned1[:], nc.vector.tensor_copy)
         weave(grouped2[:], turned2[:, :, NARROW_ROWS], nc.vector.tensor_copy)
-        weave(grouped_w[:], turned_w[:], nc.scalar.copy)
-        quantise(grouped1[:], Q)
-        quantise(grouped_w[:], 0)
+        weave(grouped_w1[:, :I], turned_w[:], nc.scalar.copy)
+        quantise(grouped_w1[:], 0)
         quantise(grouped2[:], Q + 2 * P)
         grouped3 = keep.tile([P, I], BF16, name="grouped3", align_bytes=64)
         weave(grouped3[:], turned3[:], nc.scalar.copy)

@@ -143,12 +143,6 @@ def tile_attend_vqattention_kernel(tc, query, book_words, book_scales, size, val
                 stop=True,
             )
 
-        def store(acc, feature, copy_out):
-            width = acc.shape[1]
-            result = keep.tile([P, width], F32, name=f"result{feature}")
-            copy_out(out=result[:], in_=acc[:])
-            nc.sync.dma_start(out=out[:, feature : feature + width], in_=result[:])
-
         picked = gather(keep.tile([P, I], F32, name="picked"), scores, code_list, 20)
         neg_max = keep.tile([P, 1], F32, name="neg_max")
         probs = shared.tile([P, I], F32, name="probs", offset=4 * POOL_BYTES + 1024)
@@ -209,7 +203,9 @@ def tile_attend_vqattention_kernel(tc, query, book_words, book_scales, size, val
         out4 = psum.tile([P, P], F32, name="out4", tag="bank5")
         multiply(out4[:], EARLY)
         quantise(grouped5[:], Q + E - HALF)
-        store(out4, EARLY, nc.vector.tensor_copy)
+        last = keep.tile([P, E - EARLY], F32, name="last")
+        nc.vector.tensor_copy(out=last[:, :P], in_=out4[:])
         out5 = psum.tile([P, HALF], F32, name="out5")
         multiply(out5[:], E - HALF)
-        store(out5, E - HALF, nc.scalar.copy)
+        nc.scalar.copy(out=last[:, P:], in_=out5[:])
+        nc.sync.dma_start(out=out[:, EARLY:], in_=last[:])

@@ -61,9 +61,9 @@ def tile_attend_vqattention_kernel(tc, query, book_words, book_scales, size, val
         nc.sync.dma_start(code_list[:], offs)
         nc.sync.dma_start(out=first[:], in_=vals[0:P, :])
         nc.sync.dma_start(token_list[:], offs2)
-        nc.sync.dma_start(out=narrow[NARROW_ROWS, :], in_=vals[2 * P : EARLY, :])
+        nc.sync.dma_start(out=narrow[NARROW_ROWS, :], in_=vals[P : P + HALF, :])
         nc.sync.dma_start(out=size_chunks[SIZE_ROWS, :], in_=size[0].rearrange("(c m) -> c m", m=P))
-        nc.sync.dma_start(out=third[:], in_=vals[P : 2 * P, :])
+        nc.sync.dma_start(out=third[:], in_=vals[P + HALF : EARLY, :])
         nc.sync.dma_start(out=fourth[:], in_=vals[EARLY : EARLY + P, :])
         make_identity(nc, ident[:])
 
@@ -127,17 +127,17 @@ def tile_attend_vqattention_kernel(tc, query, book_words, book_scales, size, val
         codes = shared.tile([P, Q + E], U32, name="codes", offset=2 * POOL_BYTES, align_bytes=64)
         plane = keep.tile([P, Q + E], U8, name="plane", align_bytes=64)
 
-        def quantise(grouped, column):
+        def quantise(grouped, column, codes=codes):
             cols = slice(column, column + grouped.shape[1] // PACK)
             nc.vector.quantize_mx(out=codes[:, cols].bitcast(FP8X4), scales=plane[:, cols], in_=grouped)
 
-        def multiply(acc, feature):
+        def multiply(acc, feature, moving=codes):
             cols = slice(Q + feature, Q + feature + acc.shape[1])
             nc.tensor.matmul_mx(
                 out=acc,
                 lhsT=codes[:, :Q].bitcast(FP8X4),
                 lhsT_scale=plane[:, :Q],
-                rhs=codes[:, cols].bitcast(FP8X4),
+                rhs=moving[:, cols].bitcast(FP8X4),
                 rhs_scale=plane[:, cols],
                 start=True,
                 stop=True,
@@ -180,26 +180,31 @@ def tile_attend_vqattention_kernel(tc, query, book_words, book_scales, size, val
         weave(grouped_w1[:, I:], turned1[:], nc.vector.tensor_copy)
         weave(grouped2[:], turned2[:, :, NARROW_ROWS], nc.vector.tensor_copy)
         weave(grouped_w1[:, :I], turned_w[:], nc.scalar.copy)
-        quantise(grouped_w1[:], 0)
-        quantise(grouped2[:], Q + 2 * P)
+        quantise(grouped_w1[:, I:], Q)
+        quantise(grouped2[:], Q + P)
+        quantise(grouped_w1[:, :I], 0)
         grouped3 = keep.tile([P, I], BF16, name="grouped3", align_bytes=64)
         weave(grouped3[:], turned3[:], nc.scalar.copy)
-        quantise(grouped3[:], Q + P)
-        early_out = psum.tile([P, EARLY], F32, name="early_out", tag="bank4")
-        multiply(early_out[:, : 2 * P], 0)
-        multiply(early_out[:, 2 * P :], 2 * P)
-        gathered4 = gather(keep.tile([P, I], BF16, name="gathered4", align_bytes=64), fourth, token_list, 12)
+        early_out = psum.tile([P, P + HALF], F32, name="early_out", tag="bank4")
+        multiply(early_out[:, :P], 0)
+        multiply(early_out[:, P:], P)
+        gathered4 = gather(keep.tile([P, I], BF16, name="gathered4", align_bytes=64), fourth, token_list, SHARE)
         turned4 = turn("bank3", gathered4)
         gathered5 = gather(keep.tile([P, I], BF16, name="gathered5", align_bytes=64), first, token_list, SHARE)
         turned5 = turn("bank0", gathered5)
         grouped4 = shared.tile([P, I], BF16, name="grouped4", offset=0, align_bytes=64)
         weave(grouped4[:], turned4[:], nc.scalar.copy)
+        codes3 = shared.tile([P, Q + EARLY], U32, name="codes3", offset=4096, align_bytes=64)
+        quantise(grouped3[:], Q + P + HALF, codes3)
         early_result = shared.tile([P, EARLY], F32, name="early_result", offset=1024)
-        nc.vector.tensor_copy(out=early_result[:], in_=early_out[:])
-        nc.sync.dma_start(out=out[:, :EARLY], in_=early_result[:])
+        nc.vector.tensor_copy(out=early_result[:, : P + HALF], in_=early_out[:])
+        out3 = psum.tile([P, P], F32, name="out3", tag="bank1")
+        multiply(out3[:], P + HALF, codes3)
         quantise(grouped4[:], Q + EARLY)
         grouped5 = keep.tile([P, I // 2], BF16, name="grouped5", align_bytes=64)
         weave(grouped5[:], turned5[:, :, NARROW_ROWS], nc.scalar.copy)
+        nc.scalar.copy(out=early_result[:, P + HALF :], in_=out3[:])
+        nc.sync.dma_start(out=out[:, :EARLY], in_=early_result[:])
         out4 = psum.tile([P, P], F32, name="out4", tag="bank5")
         multiply(out4[:], EARLY)
         quantise(grouped5[:], Q + E - HALF)

@@ -37,7 +37,7 @@ def tile_attend_vqattention_kernel(tc, query, book_words, book_scales, size, val
 
         code_list = keep.tile([P, LIST_COLS], U16, name="code_list")
         token_list = keep.tile([P, LIST_COLS], U16, name="token_list")
-        q_raw = keep.tile([P, PACK, Q], F32, name="q_raw")
+        q_raw = shared.tile([P, PACK, Q], F32, name="q_raw", offset=3 * POOL_BYTES - 1024)
         book_codes = keep.tile([P, C], U32, name="book_codes", align_bytes=64)
         book_plane = keep.tile([P, C], U8, name="book_plane", align_bytes=64)
         size_chunks = shared.tile([P, P], F32, name="size_chunks", offset=4 * POOL_BYTES + 768)
@@ -49,7 +49,7 @@ def tile_attend_vqattention_kernel(tc, query, book_words, book_scales, size, val
 
         nc.vector.memset(book_plane[:].bitcast(I32), 0)
         nc.vector.memset(narrow[:].bitcast(I32), 0)
-        nc.gpsimd.memset(size_chunks[:], 0.0)
+        nc.vector.memset(size_chunks[:], 0.0)
         scale_rows = book_scales[0].bitcast(I32)
         nc.sync.dma_start(out=q_raw[:], in_=query.rearrange("(p j) q -> p j q", j=PACK))
         nc.sync.dma_start(
@@ -57,7 +57,8 @@ def tile_attend_vqattention_kernel(tc, query, book_words, book_scales, size, val
             in_=book_words[0].rearrange("p c t -> p (c t)").bitcast(I32),
         )
         for r in range(4):
-            nc.sync.dma_start(out=book_plane[r:P:32, :].bitcast(I32), in_=scale_rows[r:16:4, :])
+            queue = nc.sync if r < 2 else nc.scalar
+            queue.dma_start(out=book_plane[r:P:32, :].bitcast(I32), in_=scale_rows[r:16:4, :])
         nc.sync.dma_start(code_list[:], offs)
         nc.sync.dma_start(out=first[:], in_=vals[0:P, :])
         nc.sync.dma_start(token_list[:], offs2)

@@ -209,9 +209,11 @@ def tile_attend_vqattention_kernel(tc, query, book_words, book_scales, size, val
         out4 = psum.tile([P, P], F32, name="out4", tag="bank5")
         multiply(out4[:], EARLY)
         quantise(grouped5[:], Q + E - HALF)
-        last = keep.tile([P, E - EARLY], F32, name="last")
-        nc.vector.tensor_copy(out=last[:, :P], in_=out4[:])
+        middle = keep.tile([P, P], F32, name="middle")
+        nc.vector.tensor_copy(out=middle[:], in_=out4[:])
         out5 = psum.tile([P, HALF], F32, name="out5")
         multiply(out5[:], E - HALF)
-        nc.scalar.copy(out=last[:, P:], in_=out5[:])
-        nc.sync.dma_start(out=out[:, EARLY:], in_=last[:])
+        last = keep.tile([P, HALF], F32, name="last")
+        nc.scalar.copy(out=last[:], in_=out5[:])
+        nc.scalar.dma_start(out=out[:, E - HALF :], in_=last[:])
+        nc.sync.dma_start(out=out[:, EARLY : E - HALF], in_=middle[:])

@@ -21,11 +21,13 @@ PACK = 4
 HALF = P // 2
 CHUNKS = I // P
 LIST_COLS = I // 16
-SHARE = 16
 NARROW_ROWS = slice(32, 96)
-EARLY = 2 * P + HALF
 SIZE_ROWS = slice(8, P, 36)
 POOL_BYTES = 4 * T
+SCORE_SHARE = 20
+SHARE3 = 28
+SHARE4 = 8
+SHARE5 = 16
 
 
 def tile_attend_vqattention_kernel(tc, query, book_words, book_scales, size, vals, offs, offs2, out):
@@ -37,19 +39,20 @@ def tile_attend_vqattention_kernel(tc, query, book_words, book_scales, size, val
 
         code_list = keep.tile([P, LIST_COLS], U16, name="code_list")
         token_list = keep.tile([P, LIST_COLS], U16, name="token_list")
-        q_raw = shared.tile([P, PACK, Q], F32, name="q_raw", offset=3 * POOL_BYTES - 1024)
+        q_raw = keep.tile([P, PACK, Q], F32, name="q_raw")
         book_codes = keep.tile([P, C], U32, name="book_codes", align_bytes=64)
         book_plane = keep.tile([P, C], U8, name="book_plane", align_bytes=64)
-        size_chunks = shared.tile([P, P], F32, name="size_chunks", offset=4 * POOL_BYTES + 768)
+        size_chunks = shared.tile([P, P], F32, name="size_chunks", offset=2 * POOL_BYTES)
         first = shared.tile([P, T], F32, name="first", offset=0)
-        narrow = shared.tile([P, T], F32, name="narrow", offset=POOL_BYTES)
-        third = shared.tile([P, T], F32, name="third", offset=2 * POOL_BYTES)
-        fourth = shared.tile([P, T], F32, name="fourth", offset=3 * POOL_BYTES)
+        second = keep.tile([P, T], F32, name="second")
+        third = shared.tile([P, T], F32, name="third", offset=POOL_BYTES)
+        narrow = keep.tile([P, T], F32, name="narrow")
         ident = keep.tile([P, P], F32, name="ident")
 
+        nc.gpsimd.memset(size_chunks[:], 0.0)
+        nc.gpsimd.dma_start(out=size_chunks[SIZE_ROWS, :], in_=size[0].rearrange("(c m) -> c m", m=P))
         nc.vector.memset(book_plane[:].bitcast(I32), 0)
         nc.vector.memset(narrow[:].bitcast(I32), 0)
-        nc.vector.memset(size_chunks[:], 0.0)
         scale_rows = book_scales[0].bitcast(I32)
         nc.sync.dma_start(out=q_raw[:], in_=query.rearrange("(p j) q -> p j q", j=PACK))
         nc.sync.dma_start(
@@ -60,12 +63,11 @@ def tile_attend_vqattention_kernel(tc, query, book_words, book_scales, size, val
             queue = nc.sync if r < 2 else nc.scalar
             queue.dma_start(out=book_plane[r:P:32, :].bitcast(I32), in_=scale_rows[r:16:4, :])
         nc.sync.dma_start(code_list[:], offs)
-        nc.sync.dma_start(out=first[:], in_=vals[0:P, :])
+        nc.sync.dma_start(out=first[:], in_=vals[P : 2 * P, :])
         nc.sync.dma_start(token_list[:], offs2)
-        nc.sync.dma_start(out=narrow[NARROW_ROWS, :], in_=vals[P : P + HALF, :])
-        nc.sync.dma_start(out=size_chunks[SIZE_ROWS, :], in_=size[0].rearrange("(c m) -> c m", m=P))
-        nc.sync.dma_start(out=third[:], in_=vals[P + HALF : EARLY, :])
-        nc.sync.dma_start(out=fourth[:], in_=vals[EARLY : EARLY + P, :])
+        nc.sync.dma_start(out=second[:], in_=vals[0:P, :])
+        nc.sync.dma_start(out=third[:], in_=vals[2 * P : 3 * P, :])
+        nc.sync.dma_start(out=narrow[NARROW_ROWS, :], in_=vals[3 * P : 3 * P + HALF, :])
         make_identity(nc, ident[:])
 
         q_grouped = keep.tile([P, Q * PACK], BF16, name="q_grouped", align_bytes=64)
@@ -102,7 +104,8 @@ def tile_attend_vqattention_kernel(tc, query, book_words, book_scales, size, val
         size_turned = psum.tile([P, P], F32, name="size_turned", tag="bank5")
         nc.tensor.transpose(size_turned[:], size_chunks[:], ident[:])
 
-        def gather(picked, window, slots, vector_cols):
+        def gather(name, dtype, window, slots, vector_cols):
+            picked = keep.tile([P, I], dtype, name=name, align_bytes=64)
             cut = 16 * vector_cols
             if vector_cols > 0:
                 nc.vector.tensor_copy(out=picked[:, :cut], in_=window[:].indirect(slots[:, :vector_cols]))
@@ -111,9 +114,7 @@ def tile_attend_vqattention_kernel(tc, query, book_words, book_scales, size, val
             return picked
 
         def turn(bank, rows):
-            return turn_into(psum.tile([P, 2, P], F32, name="turned", tag=bank), rows)
-
-        def turn_into(turned, rows):
+            turned = psum.tile([P, 2, P], F32, name="turned", tag=bank)
             words = rows[:].bitcast(F32)
             for u in range(2):
                 nc.tensor.transpose(turned[:, u, :], words[:, u : 2 * P : 2], ident[:])
@@ -125,7 +126,7 @@ def tile_attend_vqattention_kernel(tc, query, book_words, book_scales, size, val
                 in_=turned.rearrange("p u r -> p r u"),
             )
 
-        codes = shared.tile([P, Q + E], U32, name="codes", offset=2 * POOL_BYTES, align_bytes=64)
+        codes = shared.tile([P, Q + E], U32, name="codes", offset=POOL_BYTES, align_bytes=64)
         plane = keep.tile([P, Q + E], U8, name="plane", align_bytes=64)
 
         def quantise(grouped, column, codes=codes):
@@ -144,14 +145,14 @@ def tile_attend_vqattention_kernel(tc, query, book_words, book_scales, size, val
                 stop=True,
             )
 
-        picked = gather(keep.tile([P, I], F32, name="picked"), scores, code_list, 20)
+        picked = gather("picked", F32, scores, code_list, SCORE_SHARE)
         neg_max = keep.tile([P, 1], F32, name="neg_max")
-        probs = shared.tile([P, I], F32, name="probs", offset=4 * POOL_BYTES + 1024)
+        probs = shared.tile([P, I], F32, name="probs", offset=2 * POOL_BYTES + 256)
         row_sum = keep.tile([P, 1], F32, name="row_sum")
-        inv_sum = shared.tile([P, 1], F32, name="inv_sum", offset=4 * POOL_BYTES + 768)
+        inv_sum = keep.tile([P, 1], F32, name="inv_sum")
         weights = keep.tile([P, I], BF16, name="weights")
         nc.vector.tensor_reduce(out=neg_max[:], in_=picked[:], axis=mybir.AxisListType.X, op=ALU.max, negate=True)
-        gathered1 = gather(keep.tile([P, I], BF16, name="gathered1"), first, token_list, 0)
+        gathered1 = gather("gathered1", BF16, first, token_list, 0)
         nc.sync.dma_start(out=first[NARROW_ROWS, :], in_=vals[E - HALF :, :])
         size_col = keep.tile([P, CHUNKS], F32, name="size_col")
         nc.scalar.copy(out=size_col[:], in_=size_turned[:, SIZE_ROWS])
@@ -159,9 +160,10 @@ def tile_attend_vqattention_kernel(tc, query, book_words, book_scales, size, val
         size_rows = psum.tile([P, I], F32, name="size_rows", tag="bank0")
         for c in range(CHUNKS):
             nc.tensor.transpose(size_rows[:, c * P : (c + 1) * P], size_col[:, c : c + 1].to_broadcast([P, P]), ident[:])
-        both = psum.tile([P, 4, P], F32, name="both", tag="bank5")
-        turned1 = turn_into(both[:, :2, :], gathered1)
-        gathered2 = gather(keep.tile([P, I], BF16, name="gathered2"), narrow, token_list, LIST_COLS)
+        turned1 = turn("bank5", gathered1)
+        grouped1 = keep.tile([P, I], BF16, name="grouped1", align_bytes=64)
+        codes1 = keep.tile([P, Q + 2 * P], U32, name="codes1", align_bytes=64)
+        weave(grouped1[:], turned1[:], nc.vector.tensor_copy)
         nc.vector.reciprocal(out=inv_sum[:], in_=row_sum[:])
         nc.vector.scalar_tensor_tensor(
             out=weights[:],
@@ -171,49 +173,45 @@ def tile_attend_vqattention_kernel(tc, query, book_words, book_scales, size, val
             op0=ALU.mult,
             op1=ALU.mult,
         )
-
-        turned2 = turn_into(both[:, 2:, :], gathered2)
+        quantise(grouped1[:], Q + P, codes1)
+        grouped_w2 = keep.tile([P, 2 * I], BF16, name="grouped_w2", align_bytes=64)
+        gathered2 = gather("gathered2", BF16, second, token_list, 0)
         turned_w = turn("bank2", weights)
-        gathered3 = gather(keep.tile([P, I], BF16, name="gathered3"), third, token_list, 8)
-        turned3 = turn("bank1", gathered3)
-        grouped_w1 = shared.tile([P, 2 * I], BF16, name="grouped_w1", offset=2 * POOL_BYTES + 4096, align_bytes=64)
-        grouped2 = shared.tile([P, I // 2], BF16, name="grouped2", offset=2 * POOL_BYTES + 6144, align_bytes=64)
-        weave(grouped_w1[:, I:], turned1[:], nc.vector.tensor_copy)
-        weave(grouped2[:], turned2[:, :, NARROW_ROWS], nc.vector.tensor_copy)
-        weave(grouped_w1[:, :I], turned_w[:], nc.scalar.copy)
-        quantise(grouped_w1[:, I:], Q)
-        quantise(grouped2[:], Q + P)
-        quantise(grouped_w1[:, :I], 0)
-        grouped3 = keep.tile([P, I], BF16, name="grouped3", align_bytes=64)
-        weave(grouped3[:], turned3[:], nc.scalar.copy)
-        early_out = psum.tile([P, P + HALF], F32, name="early_out", tag="bank4")
+        turned2 = turn("bank1", gathered2)
+        weave(grouped_w2[:, :I], turned_w[:], nc.scalar.copy)
+        weave(grouped_w2[:, I:], turned2[:], nc.scalar.copy)
+        gathered3 = gather("gathered3", BF16, third, token_list, SHARE3)
+        turned3 = turn("bank3", gathered3)
+        quantise(grouped_w2[:], 0)
+        early_out = psum.tile([P, 2 * P], F32, name="early_out", tag="bank4")
         multiply(early_out[:, :P], 0)
-        multiply(early_out[:, P:], P)
-        gathered4 = gather(keep.tile([P, I], BF16, name="gathered4", align_bytes=64), fourth, token_list, SHARE)
-        turned4 = turn("bank3", gathered4)
-        gathered5 = gather(keep.tile([P, I], BF16, name="gathered5", align_bytes=64), first, token_list, SHARE)
-        turned5 = turn("bank0", gathered5)
-        grouped4 = shared.tile([P, I], BF16, name="grouped4", offset=0, align_bytes=64)
-        weave(grouped4[:], turned4[:], nc.scalar.copy)
-        codes3 = shared.tile([P, Q + EARLY], U32, name="codes3", offset=4096, align_bytes=64)
-        quantise(grouped3[:], Q + P + HALF, codes3)
-        early_result = shared.tile([P, EARLY], F32, name="early_result", offset=1024)
-        nc.vector.tensor_copy(out=early_result[:, : P + HALF], in_=early_out[:])
-        out3 = psum.tile([P, P], F32, name="out3", tag="bank1")
-        multiply(out3[:], P + HALF, codes3)
-        quantise(grouped4[:], Q + EARLY)
+        multiply(early_out[:, P:], P, codes1)
+        gathered4 = gather("gathered4", BF16, narrow, token_list, SHARE4)
+        turned4 = turn("bank0", gathered4)
+        gathered5 = gather("gathered5", BF16, first, token_list, SHARE5)
+        turned5 = turn("bank5", gathered5)
+        early = shared.tile([P, 2 * P], F32, name="early", offset=2048)
+        nc.vector.tensor_copy(out=early[:], in_=early_out[:])
+        nc.sync.dma_start(out=out[:, : 2 * P], in_=early[:])
+        grouped3 = shared.tile([P, I], BF16, name="grouped3", offset=0, align_bytes=64)
+        grouped4 = shared.tile([P, I // 2], BF16, name="grouped4", offset=1024, align_bytes=64)
         grouped5 = keep.tile([P, I // 2], BF16, name="grouped5", align_bytes=64)
+        weave(grouped3[:], turned3[:], nc.scalar.copy)
+        quantise(grouped3[:], Q + 2 * P)
+        weave(grouped4[:], turned4[:, :, NARROW_ROWS], nc.scalar.copy)
+        quantise(grouped4[:], Q + 3 * P)
         weave(grouped5[:], turned5[:, :, NARROW_ROWS], nc.scalar.copy)
-        nc.scalar.copy(out=early_result[:, P + HALF :], in_=out3[:])
-        nc.sync.dma_start(out=out[:, :EARLY], in_=early_result[:])
-        out4 = psum.tile([P, P], F32, name="out4", tag="bank5")
-        multiply(out4[:], EARLY)
+        out3 = psum.tile([P, P], F32, name="out3", tag="bank1")
+        multiply(out3[:], 2 * P)
+        out4 = psum.tile([P, HALF], F32, name="out4", tag="bank2")
+        multiply(out4[:], 3 * P)
+        middle = keep.tile([P, P + HALF], F32, name="middle")
+        nc.scalar.copy(out=middle[:, :P], in_=out3[:])
         quantise(grouped5[:], Q + E - HALF)
-        middle = keep.tile([P, P], F32, name="middle")
-        nc.vector.tensor_copy(out=middle[:], in_=out4[:])
-        out5 = psum.tile([P, HALF], F32, name="out5")
+        nc.vector.tensor_copy(out=middle[:, P:], in_=out4[:])
+        nc.sync.dma_start(out=out[:, 2 * P : E - HALF], in_=middle[:])
+        out5 = psum.tile([P, HALF], F32, name="out5", tag="bank6")
         multiply(out5[:], E - HALF)
         last = keep.tile([P, HALF], F32, name="last")
         nc.scalar.copy(out=last[:], in_=out5[:])
-        nc.scalar.dma_start(out=out[:, E - HALF :], in_=last[:])
-        nc.sync.dma_start(out=out[:, EARLY : E - HALF], in_=middle[:])
+        nc.sync.dma_start(out=out[:, E - HALF :], in_=last[:])

@@ -24,9 +24,9 @@ LIST_COLS = I // 16
 NARROW_ROWS = slice(32, 96)
 SIZE_ROWS = slice(8, P, 36)
 POOL_BYTES = 4 * T
-SCORE_SHARE = 20
+SCORE_SHARE = 16
 SHARE3 = 28
-SHARE4 = 8
+SHARE4 = 10
 SHARE5 = 16
 
 
@@ -79,7 +79,7 @@ def tile_attend_vqattention_kernel(tc, query, book_words, book_scales, size, val
         )
         nc.vector.quantize_mx(out=q_codes[:].bitcast(FP8X4), scales=q_plane[:], in_=q_grouped[:])
 
-        scores = keep.tile([P, C], F32, name="scores", align_bytes=64)
+        scores = shared.tile([P, C], F32, name="scores", offset=3 * POOL_BYTES + 2048, align_bytes=64)
         pieces = (
             (0, 256, nc.vector.tensor_copy),
             (256, 512, nc.scalar.copy),
@@ -104,8 +104,7 @@ def tile_attend_vqattention_kernel(tc, query, book_words, book_scales, size, val
         size_turned = psum.tile([P, P], F32, name="size_turned", tag="bank5")
         nc.tensor.transpose(size_turned[:], size_chunks[:], ident[:])
 
-        def gather(name, dtype, window, slots, vector_cols):
-            picked = keep.tile([P, I], dtype, name=name, align_bytes=64)
+        def gather(picked, window, slots, vector_cols):
             cut = 16 * vector_cols
             if vector_cols > 0:
                 nc.vector.tensor_copy(out=picked[:, :cut], in_=window[:].indirect(slots[:, :vector_cols]))
@@ -145,25 +144,25 @@ def tile_attend_vqattention_kernel(tc, query, book_words, book_scales, size, val
                 stop=True,
             )
 
-        picked = gather("picked", F32, scores, code_list, SCORE_SHARE)
+        picked = keep.tile([P, I], F32, name="picked")
+        gather(picked, scores, code_list, SCORE_SHARE)
         neg_max = keep.tile([P, 1], F32, name="neg_max")
         probs = shared.tile([P, I], F32, name="probs", offset=2 * POOL_BYTES + 256)
-        row_sum = keep.tile([P, 1], F32, name="row_sum")
+        row_sum = shared.tile([P, 1], F32, name="row_sum", offset=3 * POOL_BYTES)
         inv_sum = keep.tile([P, 1], F32, name="inv_sum")
         weights = keep.tile([P, I], BF16, name="weights")
         nc.vector.tensor_reduce(out=neg_max[:], in_=picked[:], axis=mybir.AxisListType.X, op=ALU.max, negate=True)
-        gathered1 = gather("gathered1", BF16, first, token_list, 0)
+        gathered1 = gather(keep.tile([P, I], BF16, name="gathered1", align_bytes=64), first, token_list, 0)
         nc.sync.dma_start(out=first[NARROW_ROWS, :], in_=vals[E - HALF :, :])
-        size_col = keep.tile([P, CHUNKS], F32, name="size_col")
-        nc.scalar.copy(out=size_col[:], in_=size_turned[:, SIZE_ROWS])
+        size_col = shared.tile([P, CHUNKS], F32, name="size_col", offset=3 * POOL_BYTES + 2048)
+        nc.vector.tensor_copy(out=size_col[:], in_=size_turned[:, SIZE_ROWS])
         nc.scalar.activation(out=probs[:], in_=picked[:], func=ACT.Exp, bias=neg_max[:], accum_out=row_sum[:])
         size_rows = psum.tile([P, I], F32, name="size_rows", tag="bank0")
         for c in range(CHUNKS):
             nc.tensor.transpose(size_rows[:, c * P : (c + 1) * P], size_col[:, c : c + 1].to_broadcast([P, P]), ident[:])
         turned1 = turn("bank5", gathered1)
-        grouped1 = keep.tile([P, I], BF16, name="grouped1", align_bytes=64)
+        grouped1 = shared.tile([P, I], BF16, name="grouped1", offset=3 * POOL_BYTES, align_bytes=64)
         codes1 = keep.tile([P, Q + 2 * P], U32, name="codes1", align_bytes=64)
-        weave(grouped1[:], turned1[:], nc.vector.tensor_copy)
         nc.vector.reciprocal(out=inv_sum[:], in_=row_sum[:])
         nc.vector.scalar_tensor_tensor(
             out=weights[:],
@@ -173,22 +172,23 @@ def tile_attend_vqattention_kernel(tc, query, book_words, book_scales, size, val
             op0=ALU.mult,
             op1=ALU.mult,
         )
+        weave(grouped1[:], turned1[:], nc.vector.tensor_copy)
         quantise(grouped1[:], Q + P, codes1)
         grouped_w2 = keep.tile([P, 2 * I], BF16, name="grouped_w2", align_bytes=64)
-        gathered2 = gather("gathered2", BF16, second, token_list, 0)
+        gathered2 = gather(keep.tile([P, I], BF16, name="gathered2", align_bytes=64), second, token_list, 0)
         turned_w = turn("bank2", weights)
-        turned2 = turn("bank1", gathered2)
+        turned2 = turn("bank3", gathered2)
         weave(grouped_w2[:, :I], turned_w[:], nc.scalar.copy)
         weave(grouped_w2[:, I:], turned2[:], nc.scalar.copy)
-        gathered3 = gather("gathered3", BF16, third, token_list, SHARE3)
-        turned3 = turn("bank3", gathered3)
+        gathered3 = gather(keep.tile([P, I], BF16, name="gathered3", align_bytes=64), third, token_list, SHARE3)
+        turned3 = turn("bank1", gathered3)
         quantise(grouped_w2[:], 0)
         early_out = psum.tile([P, 2 * P], F32, name="early_out", tag="bank4")
         multiply(early_out[:, :P], 0)
         multiply(early_out[:, P:], P, codes1)
-        gathered4 = gather("gathered4", BF16, narrow, token_list, SHARE4)
+        gathered4 = gather(keep.tile([P, I], BF16, name="gathered4", align_bytes=64), narrow, token_list, SHARE4)
         turned4 = turn("bank0", gathered4)
-        gathered5 = gather("gathered5", BF16, first, token_list, SHARE5)
+        gathered5 = gather(keep.tile([P, I], BF16, name="gathered5", align_bytes=64), first, token_list, SHARE5)
         turned5 = turn("bank5", gathered5)
         early = shared.tile([P, 2 * P], F32, name="early", offset=2048)
         nc.vector.tensor_copy(out=early[:], in_=early_out[:])
@@ -201,7 +201,7 @@ def tile_attend_vqattention_kernel(tc, query, book_words, book_scales, size, val
         weave(grouped4[:], turned4[:, :, NARROW_ROWS], nc.scalar.copy)
         quantise(grouped4[:], Q + 3 * P)
         weave(grouped5[:], turned5[:, :, NARROW_ROWS], nc.scalar.copy)
-        out3 = psum.tile([P, P], F32, name="out3", tag="bank1")
+        out3 = psum.tile([P, P], F32, name="out3", tag="bank3")
         multiply(out3[:], 2 * P)
         out4 = psum.tile([P, HALF], F32, name="out4", tag="bank2")
         multiply(out4[:], 3 * P)

@@ -25,8 +25,8 @@ NARROW_ROWS = slice(32, 96)
 SIZE_ROWS = slice(8, P, 36)
 POOL_BYTES = 4 * T
 SCORE_SHARE = 16
-SHARE3 = 28
-SHARE4 = 10
+SHARE3 = 32
+SHARE4 = 4
 SHARE5 = 16
 
 

from contextlib import ExitStack

import concourse.mybir as mybir
from concourse.masks import make_identity

D, C, T, I, Q, E = 512, 1024, 2048, 512, 128, 512
FLOPS = 2 * D * Q * C + 2 * I * Q * E

F32 = mybir.dt.float32
BF16 = mybir.dt.bfloat16
I32 = mybir.dt.int32
U32 = mybir.dt.uint32
U16 = mybir.dt.uint16
U8 = mybir.dt.uint8
FP8X4 = mybir.dt.float8_e4m3fn_x4
ALU = mybir.AluOpType
ACT = mybir.ActivationFunctionType

P = 128
PACK = 4
HALF = P // 2
CHUNKS = I // P
LIST_COLS = I // 16
NARROW_ROWS = slice(32, 96)
SIZE_ROWS = slice(8, P, 36)
POOL_BYTES = 4 * T
SCORE_SHARE = 16
SHARE3 = 32
SHARE4 = 4
SHARE5 = 16


def tile_attend_vqattention_kernel(tc, query, book_words, book_scales, size, vals, offs, offs2, out):
    nc = tc.nc
    with ExitStack() as ctx:
        keep = ctx.enter_context(tc.tile_pool(name="keep", bufs=1))
        shared = ctx.enter_context(tc.tile_pool(name="shared", bufs=1))
        psum = ctx.enter_context(tc.psum_pool(name="psum", bufs=1))

        code_list = keep.tile([P, LIST_COLS], U16, name="code_list")
        token_list = keep.tile([P, LIST_COLS], U16, name="token_list")
        q_raw = keep.tile([P, PACK, Q], F32, name="q_raw")
        book_codes = keep.tile([P, C], U32, name="book_codes", align_bytes=64)
        book_plane = keep.tile([P, C], U8, name="book_plane", align_bytes=64)
        size_chunks = shared.tile([P, P], F32, name="size_chunks", offset=2 * POOL_BYTES)
        first = shared.tile([P, T], F32, name="first", offset=0)
        second = keep.tile([P, T], F32, name="second")
        third = shared.tile([P, T], F32, name="third", offset=POOL_BYTES)
        narrow = keep.tile([P, T], F32, name="narrow")
        ident = keep.tile([P, P], F32, name="ident")

        nc.gpsimd.memset(size_chunks[:], 0.0)
        nc.gpsimd.dma_start(out=size_chunks[SIZE_ROWS, :], in_=size[0].rearrange("(c m) -> c m", m=P))
        nc.vector.memset(book_plane[:].bitcast(I32), 0)
        nc.vector.memset(narrow[:].bitcast(I32), 0)
        scale_rows = book_scales[0].bitcast(I32)
        nc.sync.dma_start(out=q_raw[:], in_=query.rearrange("(p j) q -> p j q", j=PACK))
        nc.sync.dma_start(
            out=book_codes[:].bitcast(I32),
            in_=book_words[0].rearrange("p c t -> p (c t)").bitcast(I32),
        )
        for r in range(4):
            queue = nc.sync if r < 2 else nc.scalar
            queue.dma_start(out=book_plane[r:P:32, :].bitcast(I32), in_=scale_rows[r:16:4, :])
        nc.sync.dma_start(code_list[:], offs)
        nc.sync.dma_start(out=first[:], in_=vals[P : 2 * P, :])
        nc.sync.dma_start(token_list[:], offs2)
        nc.sync.dma_start(out=second[:], in_=vals[0:P, :])
        nc.sync.dma_start(out=third[:], in_=vals[2 * P : 3 * P, :])
        nc.sync.dma_start(out=narrow[NARROW_ROWS, :], in_=vals[3 * P : 3 * P + HALF, :])
        make_identity(nc, ident[:])

        q_grouped = keep.tile([P, Q * PACK], BF16, name="q_grouped", align_bytes=64)
        q_codes = keep.tile([P, Q], U32, name="q_codes", align_bytes=64)
        q_plane = keep.tile([P, Q], U8, name="q_plane", align_bytes=64)
        nc.vector.tensor_copy(
            out=q_grouped[:].rearrange("p (c i t) -> p c t i", i=4, t=PACK),
            in_=q_raw[:].rearrange("p t (c i) -> p c t i", i=4),
        )
        nc.vector.quantize_mx(out=q_codes[:].bitcast(FP8X4), scales=q_plane[:], in_=q_grouped[:])

        scores = shared.tile([P, C], F32, name="scores", offset=3 * POOL_BYTES + 2048, align_bytes=64)
        pieces = (
            (0, 256, nc.vector.tensor_copy),
            (256, 512, nc.scalar.copy),
            (512, 768, nc.vector.tensor_copy),
            (768, 896, nc.scalar.copy),
            (896, 1024, nc.vector.tensor_copy),
        )
        for h, (start, stop, copy_out) in enumerate(pieces):
            cols = slice(start, stop)
            acc = psum.tile([P, stop - start], F32, name="score_bank", tag=f"bank{h}")
            nc.tensor.matmul_mx(
                out=acc[:],
                lhsT=q_codes[:].bitcast(FP8X4),
                lhsT_scale=q_plane[:],
                rhs=book_codes[:, cols].bitcast(FP8X4),
                rhs_scale=book_plane[:, cols],
                start=True,
                stop=True,
            )
            copy_out(out=scores[:, cols], in_=acc[:])

        size_turned = psum.tile([P, P], F32, name="size_turned", tag="bank5")
        nc.tensor.transpose(size_turned[:], size_chunks[:], ident[:])

        def gather(picked, window, slots, vector_cols):
            cut = 16 * vector_cols
            if vector_cols > 0:
                nc.vector.tensor_copy(out=picked[:, :cut], in_=window[:].indirect(slots[:, :vector_cols]))
            if vector_cols < LIST_COLS:
                nc.scalar.activation(out=picked[:, cut:], in_=window[:].indirect(slots[:, vector_cols:]), func=ACT.Copy)
            return picked

        def turn(bank, rows):
            turned = psum.tile([P, 2, P], F32, name="turned", tag=bank)
            words = rows[:].bitcast(F32)
            for u in range(2):
                nc.tensor.transpose(turned[:, u, :], words[:, u : 2 * P : 2], ident[:])
            return turned

        def weave(grouped, turned, copy_out):
            copy_out(
                out=grouped.bitcast(F32).rearrange("p (r u) -> p r u", u=2),
                in_=turned.rearrange("p u r -> p r u"),
            )

        codes = shared.tile([P, Q + E], U32, name="codes", offset=POOL_BYTES, align_bytes=64)
        plane = keep.tile([P, Q + E], U8, name="plane", align_bytes=64)

        def quantise(grouped, column, codes=codes):
            cols = slice(column, column + grouped.shape[1] // PACK)
            nc.vector.quantize_mx(out=codes[:, cols].bitcast(FP8X4), scales=plane[:, cols], in_=grouped)

        def multiply(acc, feature, moving=codes):
            cols = slice(Q + feature, Q + feature + acc.shape[1])
            nc.tensor.matmul_mx(
                out=acc,
                lhsT=codes[:, :Q].bitcast(FP8X4),
                lhsT_scale=plane[:, :Q],
                rhs=moving[:, cols].bitcast(FP8X4),
                rhs_scale=plane[:, cols],
                start=True,
                stop=True,
            )

        picked = keep.tile([P, I], F32, name="picked")
        gather(picked, scores, code_list, SCORE_SHARE)
        neg_max = keep.tile([P, 1], F32, name="neg_max")
        probs = shared.tile([P, I], F32, name="probs", offset=2 * POOL_BYTES + 256)
        row_sum = shared.tile([P, 1], F32, name="row_sum", offset=3 * POOL_BYTES)
        inv_sum = keep.tile([P, 1], F32, name="inv_sum")
        weights = keep.tile([P, I], BF16, name="weights")
        nc.vector.tensor_reduce(out=neg_max[:], in_=picked[:], axis=mybir.AxisListType.X, op=ALU.max, negate=True)
        gathered1 = gather(keep.tile([P, I], BF16, name="gathered1", align_bytes=64), first, token_list, 0)
        nc.sync.dma_start(out=first[NARROW_ROWS, :], in_=vals[E - HALF :, :])
        size_col = shared.tile([P, CHUNKS], F32, name="size_col", offset=3 * POOL_BYTES + 2048)
        nc.vector.tensor_copy(out=size_col[:], in_=size_turned[:, SIZE_ROWS])
        nc.scalar.activation(out=probs[:], in_=picked[:], func=ACT.Exp, bias=neg_max[:], accum_out=row_sum[:])
        size_rows = psum.tile([P, I], F32, name="size_rows", tag="bank0")
        for c in range(CHUNKS):
            nc.tensor.transpose(size_rows[:, c * P : (c + 1) * P], size_col[:, c : c + 1].to_broadcast([P, P]), ident[:])
        turned1 = turn("bank5", gathered1)
        grouped1 = shared.tile([P, I], BF16, name="grouped1", offset=3 * POOL_BYTES, align_bytes=64)
        codes1 = keep.tile([P, Q + 2 * P], U32, name="codes1", align_bytes=64)
        nc.vector.reciprocal(out=inv_sum[:], in_=row_sum[:])
        nc.vector.scalar_tensor_tensor(
            out=weights[:],
            in0=probs[:],
            scalar=inv_sum[:],
            in1=size_rows[:],
            op0=ALU.mult,
            op1=ALU.mult,
        )
        weave(grouped1[:], turned1[:], nc.vector.tensor_copy)
        quantise(grouped1[:], Q + P, codes1)
        grouped_w2 = keep.tile([P, 2 * I], BF16, name="grouped_w2", align_bytes=64)
        gathered2 = gather(keep.tile([P, I], BF16, name="gathered2", align_bytes=64), second, token_list, 0)
        turned_w = turn("bank2", weights)
        turned2 = turn("bank3", gathered2)
        weave(grouped_w2[:, :I], turned_w[:], nc.scalar.copy)
        weave(grouped_w2[:, I:], turned2[:], nc.scalar.copy)
        gathered3 = gather(keep.tile([P, I], BF16, name="gathered3", align_bytes=64), third, token_list, SHARE3)
        turned3 = turn("bank1", gathered3)
        quantise(grouped_w2[:], 0)
        early_out = psum.tile([P, 2 * P], F32, name="early_out", tag="bank4")
        multiply(early_out[:, :P], 0)
        multiply(early_out[:, P:], P, codes1)
        gathered4 = gather(keep.tile([P, I], BF16, name="gathered4", align_bytes=64), narrow, token_list, SHARE4)
        turned4 = turn("bank0", gathered4)
        gathered5 = gather(keep.tile([P, I], BF16, name="gathered5", align_bytes=64), first, token_list, SHARE5)
        turned5 = turn("bank5", gathered5)
        early = shared.tile([P, 2 * P], F32, name="early", offset=2048)
        nc.vector.tensor_copy(out=early[:], in_=early_out[:])
        nc.sync.dma_start(out=out[:, : 2 * P], in_=early[:])
        grouped3 = shared.tile([P, I], BF16, name="grouped3", offset=0, align_bytes=64)
        grouped4 = shared.tile([P, I // 2], BF16, name="grouped4", offset=1024, align_bytes=64)
        grouped5 = keep.tile([P, I // 2], BF16, name="grouped5", align_bytes=64)
        weave(grouped3[:], turned3[:], nc.scalar.copy)
        quantise(grouped3[:], Q + 2 * P)
        weave(grouped4[:], turned4[:, :, NARROW_ROWS], nc.scalar.copy)
        quantise(grouped4[:], Q + 3 * P)
        weave(grouped5[:], turned5[:, :, NARROW_ROWS], nc.scalar.copy)
        out3 = psum.tile([P, P], F32, name="out3", tag="bank3")
        multiply(out3[:], 2 * P)
        out4 = psum.tile([P, HALF], F32, name="out4", tag="bank2")
        multiply(out4[:], 3 * P)
        middle = keep.tile([P, P + HALF], F32, name="middle")
        nc.scalar.copy(out=middle[:, :P], in_=out3[:])
        quantise(grouped5[:], Q + E - HALF)
        nc.vector.tensor_copy(out=middle[:, P:], in_=out4[:])
        nc.sync.dma_start(out=out[:, 2 * P : E - HALF], in_=middle[:])
        out5 = psum.tile([P, HALF], F32, name="out5", tag="bank6")
        multiply(out5[:], E - HALF)
        last = keep.tile([P, HALF], F32, name="last")
        nc.scalar.copy(out=last[:], in_=out5[:])
        nc.sync.dma_start(out=out[:, E - HALF :], in_=last[:])
